import numpy as np, ml_dtypes
CORES = [25,29,65,69,153,157,193,197]
N = 8
BF = ml_dtypes.bfloat16
def gentries(a):
    return np.ascontiguousarray(a.reshape(8, 16, -1).transpose(0, 2, 1)).reshape(8, -1)
def gtable(e):
    e = np.asarray(e); return np.ascontiguousarray(e.reshape(8, -1, 16).transpose(0, 2, 1)).reshape(128, -1).astype(np.int32)
R0, I0, B0, F, CAP, RO = 256, 1152, 1536, 1024, 144, 4
def weigh(b):
    return np.add.reduce(b * (2 * np.arange(16) + 1)[:, None], axis=-2)
def parts(rng):
    return (rng.integers(0, I0, (N, 8, 16, R0)), rng.integers(0, B0, (N, 8, 16, I0)), rng.integers(0, 256, (N, 8, 16, B0)), rng.integers(0, R0, (N, 8, F)), rng.integers(0, 256, (N, 8, F)))
def pack(rc, ic, b, cur, x):
    return {"rtab": np.ascontiguousarray(rc.reshape(N, 128, R0)).astype(np.int32), "itab": np.ascontiguousarray(ic.reshape(N, 128, I0)).astype(np.int32),
            "btab": np.ascontiguousarray(b.reshape(N, 128, B0)).astype(np.float32).astype(BF), "rn0": np.stack([gtable(a) for a in cur]), "x0": np.ascontiguousarray(x).astype(np.int32)}
def heavy(rng, w):
    b = rng.integers(0, 16, w.shape[:-1] + (16,) + w.shape[-1:]); b = np.where((weigh(b) > w)[..., None, :], 0, b); rest = w - weigh(b)
    for i in range(15, -1, -1):
        a = np.minimum(255 - b[..., i, :], rest // (2 * i + 1)); b[..., i, :] += a; rest = rest - a * (2 * i + 1)
    return b
def setup_inputs(rng):
    return pack(*parts(rng))
def setup_inputs_room(rng):
    rc, ic, b, cur, x = parts(rng)
    w = weigh(b) - b[:, :, 0]; b[:, :, 0] = b[:, :, 0] // N * N + ((np.arange(B0) - w) & (N - 1))
    ic = ic // N * N + (np.arange(16) & (N - 1))[:, None]
    for a in range(N):
        for g in range(8):
            n = int(rng.choice(np.array([0, 1, CAP - 1, CAP, CAP + 1, 2 * CAP, F]))); m = int(rng.integers(0, N))
            if a == 0: m = 1; n = (CAP, CAP + 1, F, CAP - 1, 1, 0, CAP, 2 * CAP)[g]
            e = rng.permutation(np.concatenate([np.full(n, m), (m + rng.integers(1, N, F - n)) & (N - 1)]))
            d2 = ((e - np.arange(F)) & (N - 1)) + N * rng.integers(0, 16 // N, F)
            x[a, g] = (x[a, g] & 15) + 16 * d2
    return pack(rc, ic, b, cur, x)
def setup_inputs_full(rng):
    rc, ic, b, cur, x = parts(rng); m = int(rng.integers(0, N)); P = 1 << (B0 - 1).bit_length(); f = np.arange(F); k = np.arange(N); n = CAP // N
    for g in range(8):
        col = np.argsort(rng.random((N, B0 // N)), axis=1)[:, :CAP] * N + k[:, None]
        for a in range(N):
            late = np.argsort(rng.random((N, F // 2 // N)), axis=1)[:, :n] * N + k[:, None] + F // 2
            e = (m + rng.integers(1, N, F)) & (N - 1); w = ((e - f) & (N - 1)) + N * rng.integers(0, 65280 // N, F)
            c = col[(m - k) & (N - 1), a * n:(a + 1) * n]; w[late] = c + P * rng.integers(0, (65280 - c) // P + 1)
            q = rng.permutation(16 * R0)[:F]; inn = rng.permutation(I0)[:F]; blk = rng.permutation(B0)[:F]; d2 = rng.integers(0, 16, F)
            rc[a, g, q // R0, q % R0] = inn; ic[a, g, d2, inn] = blk; b[a, g][:, blk] = heavy(rng, w)
            cur[a, g] = q % R0; x[a, g] = q // R0 + 16 * d2
    return pack(rc, ic, b, cur, x)
def setup_inputs_deep(rng):
    rc, ic, b, cur, x = parts(rng)
    e = np.array([7, 6, 5, 4, 7, 6, 4, 3])[:, None, None]
    b = (b >> e) << e; x = (x >> e[:, :, 0]) << e[:, :, 0]
    b[:, 4:, 0] += 1; x[:, 4:] += 4
    return pack(rc, ic, b, cur, x)
def setup_inputs_ends(rng):
    rc, ic, b, cur, x = parts(rng); tg = [0, 1, 7, 8, 65279, 65280]; h = N // 2
    for t in range(RO):
        c = B0 + t * F; p = 1 << (c - 1).bit_length(); tg += [c - 1, c, c + 1, p - 1, p, p + c]
    b[::2, ::2] = heavy(rng, rng.choice(np.array(tg), (h, 4, B0)))
    b[::2, 1::4] = 255 * (b[::2, 1::4] & 1)
    rc[::2, 7] = (I0 - 1) * rng.integers(0, 2, (h, 16, R0)); ic[::2, 7] = (B0 - 1) * rng.integers(0, 2, (h, 16, I0)); cur[::2, 7] = (R0 - 1) * rng.integers(0, 2, (h, F))
    b[::2, 3] = np.where(rng.random((h, 1, B0)) < 0.25, 0, b[::2, 3]); b[:, 3, :, 0] = ((256 - RO) * 171) & 255
    cur[1::2, 0:6:2] = rng.integers(0, R0, (h, 3, 1)); rc[1::2, 1::4] = rng.integers(0, I0, (h, 2, 1, R0)); ic[1::2, 3] = rng.integers(0, B0, (h, 1, I0))
    b[1::2, 2] = np.take_along_axis(b[1::2, 2, :, :3], rng.integers(0, 3, (h, 1, B0)), 2)
    x[1::2, 4:6] = rng.integers(0, 256, (h, 2, 1))
    for g, z in ((6, 0), (7, int(rng.integers(1, 8)))):
        e = rng.integers(0, 256, 16); n = rng.integers(0, 256, 16)
        rest = int(weigh(n[:, None])[0]) - int(n[0]); n[0] = int(n[0]) // 8 * 8 + ((z - rest) & 7)
        old = (n - 3 * e) & 255; key = int(weigh(n[:, None])[0]) & 255
        v = int(weigh(old[:, None])[0]) & ((1 << (B0 - 1).bit_length()) - 1)
        if v >= B0: v -= B0
        c = (v + 1) % B0
        b[:, g, :, v] = e; b[1::2, g, :, c] = old; ic[1::2, g, key >> 4] = c; x[1::2, g] = key
    return pack(rc, ic, b, cur, x)
def setup_inputs_spread(rng):
    rc, ic, b, cur, x = parts(rng); k = rng.choice(np.array([1.0, 3.0, 8.0]), (N, 8, 1, 1))
    rc = np.minimum((I0 * rng.random((N, 8, 16, R0)) ** k).astype(np.int64), I0 - 1)
    ic = np.minimum((B0 * rng.random((N, 8, 16, I0)) ** k).astype(np.int64), B0 - 1)
    cur = np.minimum((R0 * rng.random((N, 8, F)) ** k[..., 0]).astype(np.int64), R0 - 1)
    b = b >> rng.integers(0, 9, (N, 8, 1, B0)); x = x >> rng.integers(0, 9, (N, 8, F))
    return pack(rc, ic, b, cur, x)
def check_inputs(d):
    bad = []
    for k, hi in (("rtab", I0 - 1), ("itab", B0 - 1), ("rn0", R0 - 1), ("x0", 255)):
        if np.min(d[k]) < 0 or np.max(d[k]) > hi: bad.append("range of " + k)
    v = np.asarray(d["btab"]).astype(np.float32)
    if not np.all((v >= 0) & (v <= 255) & (v == np.floor(v))): bad.append("whole numbers of btab")
    return bad
def reference(rtab, itab, btab, rn0, x0):
    r = rtab.astype(np.int64).reshape(N, 8, 16, R0); s = itab.astype(np.int64).reshape(N, 8, 16, I0); b = btab.astype(np.float32).astype(np.int64).reshape(N, 8, 16, B0)
    cur = np.stack([gentries(a) for a in rn0]).astype(np.int64); x = x0.astype(np.int64)
    f = np.arange(F); row = np.arange(16)[:, None]
    for t in range(RO):
        C = B0 + t * F; P = 1 << (C - 1).bit_length()
        d1 = (x & 15)[:, :, None, :]; d2 = ((x >> 4) & 15)[:, :, None, :]
        rc = np.take_along_axis(r, cur[:, :, None, :], 3)
        ic = np.take_along_axis(s, np.take_along_axis(rc, d1, 2), 3)
        old = np.take_along_axis(b, np.take_along_axis(ic, d2, 2), 3)
        h = weigh(old)
        to = (h + f) & (N - 1); v = h & (P - 1); v = np.where(v >= C, v - C, v)
        ok = np.zeros(to.shape, bool)
        for q in range(N):
            m = (to == q).astype(np.int64)
            ok |= (m == 1) & (np.add.accumulate(m, axis=2) - m < CAP)
        far = b[to[:, :, None, :], np.arange(8)[:, None, None], row, v[:, :, None, :]]
        far = np.where(ok[:, :, None, :], far, 0)
        new = (old + 3 * far + t) & 255
        ic = np.where(row == d2, B0 + t * F + f, ic); rc = np.where(row == d1, I0 + t * F + f, rc)
        b = np.concatenate([b, new], axis=3); s = np.concatenate([s, ic], axis=3); r = np.concatenate([r, rc], axis=3)
        x = weigh(new)
        cur = R0 + t * F + np.where((x & 7) == 0, (x >> 3) & (F - 1), f)
    return {"yb": new.reshape(N, 128, F).astype(np.float32).astype(BF), "yi": ic.reshape(N, 128, F).astype(np.float32), "yn": cur.astype(np.float32)}

@@ -1,0 +1,570 @@
+from concourse.bass import DstId, RemoteDMATransfer
+from concourse.mybir import AluOpType, ActivationFunctionType
+
+A = AluOpType
+AF = ActivationFunctionType
+N, R0, I0, B0, F, CAP, RO = 8, 256, 1152, 1536, 1024, 144, 4
+CM = B0 + 3 * F
+Z0 = 16
+W1 = R0 + I0 + 128
+W2 = 192
+TW = 256
+LOW = 8192.0
+QB = 49152.0
+PE_SLOTS = (4, 5, 6, 7)
+TURN = (6, 7)
+PRE = 1
+
+SB = lambda n, d="float32", p=128: ("sbuf", [p, n], d)
+BF, I32, U16 = "bfloat16", "int32", "uint16"
+SCRATCH = {
+    "ft": SB(Z0 + 8 * CM, BF), "tm": SB(16 * TW), "it": SB(I0 + 4096), "rt": SB(R0), "rca": SB(F), "rcb": SB(F),
+    "p1": SB(F), "p2": SB(F), "mk": SB(F, "float16"), "old": SB(F, BF), "far": SB(F, BF), "qn": SB(F, BF),
+    "hr": SB(R0, I32), "hi": SB(I0, I32), "hn": SB(64, I32), "hb": SB(B0, BF), "hx": SB(F, I32, 8), "hxb": SB(F, BF, 8),
+    "m1": SB(W1, U16), "m2": SB(W2, U16), "n1": SB(W1, U16), "n2": SB(W2, U16),
+    "jj": SB(F), "pi": SB(8, I32), "col": SB(16),
+    "zw": SB(144, BF), "zw3": SB(144, BF), "zs": SB(144, "float16"), "z8": SB(144, BF, 8),
+    "id1": SB(256, BF), "id3": SB(128, BF), "idh": SB(128, BF), "bo": SB(128, BF), "lo": SB(128, BF),
+    "rst": SB(512, BF), "fl": SB(64), "fm": SB(128), "fah": SB(64), "fao": SB(64), "et": SB(16), "mc": SB(16), "bc": SB(16),
+    "cq": SB(128, BF), "oh": SB(512, BF), "sc": SB(512, BF), "cm": SB(512, BF),
+    "wki": SB(64, I32), "wkf": SB(64), "kb": SB(128, I32), "kf": SB(128), "ko": SB(128, U16), "kd": SB(128, U16),
+    "wj": SB(64, I32), "sb": SB(128, I32), "sa": SB(192), "so": SB(64, U16), "io_": SB(64, U16), "bo_": SB(64, U16),
+    "hv": SB(256, I32), "of": SB(320), "fo": SB(64, U16), "yu": SB(F, U16), "yb_": SB(F, BF),
+}
+for _k in ("A0", "A1", "L", "K", "Q", "X0", "X1", "O"):
+    SCRATCH["ps" + _k] = ("psum", [128, 512], "float32")
+MSG = {"b": (B0 // 8, BF), "m": (W1 // 8, U16), "k": (W2 // 8, U16), "i": (F // 8, U16), "y": (F // 8, BF), "n": (F // 128, "float32")}
+for _k, (_n, _d) in MSG.items():
+    SCRATCH["s_" + _k] = ("dram", [N, 128, _n], _d)
+    SCRATCH["l_" + _k] = ("dram", [N, 128, _n], _d)
+SEMAPHORES = ["cv", "cs", "ct", "cg"] + ["d%d" % i for i in range(40)] + ["arr_" + k for k in MSG] + ["out_" + k for k in MSG]
+
+
+def routes(T, topo):
+    used = set(T.cores)
+    way = {}
+    world = range(128 * (1 + max(topo.host(c) for c in T.cores)))
+    for a in T.cores:
+        for b in T.cores:
+            if a == b or topo.may_write(a, b):
+                way[a, b] = None
+                continue
+            pool = topo.cores_of(a) if topo.host(a) == topo.host(b) else [c for c in world if topo.mates(c, b)]
+            pool = [c for c in pool if c not in used and topo.die(c) == topo.die(a) and topo.may_write(a, c) and topo.may_write(c, b)]
+            way[a, b] = pool[0]
+            used.add(pool[0])
+    return way
+
+
+def bits(es):
+    return sum(1 << e for e in es)
+
+
+def first_masks(a, T, topo, way):
+    hops = [(b, way[a, b] if way[a, b] is not None else b) for b in T.cores if b != a]
+    off = [h for h in hops if h[1] not in topo.cores_of(a)]
+    on = [h for h in hops if h[1] in topo.cores_of(a)]
+    eoff = topo.engines(a, off[0][1])
+    eon = [e for e in topo.engines(a, on[0][1]) if e not in eoff]
+    out = {}
+    for hs, es in ((off, eoff), (on, eon)):
+        n = 1
+        while 2 * n * len(hs) <= len(es):
+            n *= 2
+        for i, h in enumerate(hs):
+            out[h[0]] = es[i * n:(i + 1) * n]
+    return out
+
+
+def relay_engines(c, b, topo):
+    return topo.engines(c, b)[::2]
+
+
+def relay_program(g, core, T, topo, way):
+    pair = [k for k, v in way.items() if v == core]
+    if not pair:
+        return
+    a, b = pair[0]
+    n_in = len(first_masks(a, T, topo, way)[b])
+    es = relay_engines(core, b, topo)
+    rid, pid = topo.addr(b, core)
+    slot = T.rank_of(a)
+    for k in MSG:
+        g.wait_ge(T.sem["arr_" + k], n_in)
+        g.remote_dma(T["l_" + k][slot], T["l_" + k][slot], T.sem["arr_" + k], T.sem["out_" + k], pid, rid, bits(es))
+    for k in MSG:
+        g.wait_ge(T.sem["out_" + k], len(es))
+
+
+def rank_program(g, core, T, topo):
+    way = routes(T, topo)
+    rank = T.rank_of(core)
+    if rank is None:
+        relay_program(g, core, T, topo, way)
+        return
+
+    Q = {"v": g.vector, "s": g.scalar, "t": g.tensor, "g": g, "y": g.sync}
+    known = {q: {} for q in Q}
+    count = {"cv": 0, "cs": 0, "ct": 0, "cg": 0}
+    log = {}
+    totals = {}
+    nd = [0]
+
+    def V(name, lo=0, hi=None, step=1, p=None):
+        t = T[name]
+        hi = t.shape[1] if hi is None else hi
+        ps = slice(None) if p is None else slice(*p)
+        return (t[ps, lo:hi] if step == 1 else t[ps, lo:hi:step], [(name, lo, hi)])
+
+    def D(name, lo=0, hi=N):
+        return (T[name][lo] if hi == lo + 1 else T[name][lo:hi], [(name, lo, hi)])
+
+    def X(ap):
+        return (ap, [])
+
+    def G(win, off):
+        return (win[0].indirect(off[0]), win[1] + off[1])
+
+    def need(q, tok):
+        sem, val, clock = tok
+        if known[q].get(sem, 0) >= val:
+            return
+        Q[q].wait_ge(T.sem[sem], val)
+        for s, v in clock.items():
+            if known[q].get(s, 0) < v:
+                known[q][s] = v
+        known[q][sem] = val
+
+    def order(q, reads, writes):
+        toks = []
+        for regs, wr in ((reads, False), (writes, True)):
+            for name, lo, hi in regs:
+                ps = name.startswith("ps")
+                for (l2, h2, w2, q2, tok) in log.get(name, []):
+                    if (q2 != q) if ps else ((wr or w2) and lo < h2 and l2 < hi):
+                        toks.append(tok)
+        toks.sort(key=lambda t: -t[1])
+        for tok in toks:
+            need(q, tok)
+
+    def note(q, reads, writes, tok):
+        for regs, wr in ((reads, False), (writes, True)):
+            for name, lo, hi in regs:
+                old = log.get(name, [])
+                if wr and q != "dma" and not name.startswith("ps"):
+                    old = [e for e in old if not (lo <= e[0] and e[1] <= hi)]
+                old.append((lo, hi, wr, q, tok))
+                log[name] = old
+
+    def ap(v):
+        return v[0] if isinstance(v, tuple) else v
+
+    def run(q, out, ins, call):
+        rd = [r for v in ins if isinstance(v, tuple) for r in v[1]]
+        order(q, rd, out[1])
+        sem = "c" + q
+        call().then_inc(T.sem[sem], 1)
+        count[sem] += 1
+        note(q, rd, out[1], (sem, count[sem], dict(known[q])))
+
+    def ts(out, x, s1, op0, s2=None, op1=None):
+        if op1 is None:
+            run("v", out, [x, s1], lambda: g.vector.tensor_scalar(out[0], x[0], ap(s1), None, op0))
+        else:
+            run("v", out, [x, s1, s2], lambda: g.vector.tensor_scalar(out[0], x[0], ap(s1), ap(s2), op0, op1))
+
+    def tt(out, x, y, op):
+        run("v", out, [x, y], lambda: g.vector.tensor_tensor(out[0], x[0], y[0], op))
+
+    def cp(out, x):
+        run("v", out, [x], lambda: g.vector.tensor_copy(out[0], x[0]))
+
+    def ms(out, c):
+        run("v", out, [], lambda: g.vector.memset(out[0], c))
+
+    def act(out, x, scale=1.0, bias=0.0, func=AF.Identity):
+        run("s", out, [x, scale, bias], lambda: g.scalar.activation(out[0], x[0], func, bias=ap(bias), scale=ap(scale)))
+
+    def sel(out, x, pattern, op, fill_, base, ch):
+        run("g", out, [x], lambda: g.affine_select(out[0], x[0], pattern, op, fill_, base, ch))
+
+    def iota(out, pattern, base=0):
+        run("g", out, [], lambda: g.iota(out[0], pattern, base, 0, allow_small_or_imprecise_dtypes=True))
+
+    def mm(items):
+        rd = sorted(set(r for it in items for r in it[1][1] + it[2][1]))
+        wr = sorted(set(r for it in items for r in it[0][1]))
+        order("t", rd, wr)
+        last = None
+        for o, l, r, a, b in items:
+            last = g.tensor.matmul(o[0], l[0], r[0], a, b)
+        last.then_inc(T.sem["ct"], 1)
+        count["ct"] += 1
+        note("t", rd, wr, ("ct", count["ct"], dict(known["t"])))
+
+    def dma(items):
+        sem = "d%d" % nd[0]
+        nd[0] += 1
+        clock = {}
+        for q, o, i in items:
+            order(q, i[1], o[1])
+            Q[q].dma_start(o[0], i[0]).then_inc(T.sem[sem], 16)
+            for s, v in known[q].items():
+                clock[s] = max(v, clock.get(s, 0))
+        totals[sem] = 16 * len(items)
+        for q, o, i in items:
+            note("dma", i[1], o[1], (sem, totals[sem], clock))
+
+    masks = first_masks(core, T, topo, way)
+
+    def send(k):
+        order("g", [("s_" + k, 0, N)], [])
+        trs = []
+        for j, b in enumerate(T.cores):
+            if b == core:
+                continue
+            hop = way[core, b] if way[core, b] is not None else b
+            rid, pid = topo.addr(hop, core)
+            trs.append(RemoteDMATransfer(dst_ids=[DstId(rid=rid, pnc=pid)], dma_engine_mask=bits(masks[b]),
+                                         remote_sem=T.sem["arr_" + k], src=T["s_" + k][j], dst=T["l_" + k][rank]))
+        g.remote_dma_fused(trs, local_sem=T.sem["out_" + k])
+        totals["out_" + k] = sum(len(m) for m in masks.values())
+
+    n_arr = 0
+    for a in T.cores:
+        if a != core:
+            n_arr += len(first_masks(a, T, topo, way)[core]) if way[a, core] is None else len(relay_engines(way[a, core], core, topo))
+    for k in MSG:
+        totals["arr_" + k] = n_arr
+        for a in range(N):
+            if a != rank:
+                note("far", [], [("l_" + k, a, a + 1)], ("arr_" + k, n_arr, {}))
+    own = (16 * rank, 16 * rank + 16)
+
+    def stage(k, src, rows=None):
+        dma([("y", D("s_" + k), V(src, p=rows))])
+        dma([("y", D("l_" + k, rank, rank + 1), V(src, p=own if rows is None else (own[0], own[0] + 1)))])
+        send(k)
+
+    dma([("s", V("hx"), X(T.x0[:]))])
+    dma([("y", V("hn"), X(T.rn0[:])), ("s", V("hr"), X(T.rtab[:]))])
+    dma([("y", D("s_b"), X(T.btab[:]))])
+    dma([("y", V("hi"), X(T.itab[:]))])
+    dma([("y", V("hb"), X(T.btab[:]))])
+    dma([("y", D("l_b", rank, rank + 1), X(T.btab[own[0]:own[1], :]))])
+
+    run("g", V("pi", 0, 1), [], lambda: g.iota(T.pi[:, 0:1], [[0, 1]], 0, 1))
+    iota(V("jj", 0, TW), [[1, TW]])
+    send("b")
+    C_ = lambda i, p=None: V("col", i, i + 1, p=p)
+    P_, R_, G16, ZC, WT, WT3, Z8C, GA = range(8)
+    ms(V("rst"), 1.0)
+    ms(V("lo"), -1.0)
+    ms(V("ft", 0, Z0), 0.0)
+    ts(V("pi", 1, 2), V("pi", 0, 1), 15, A.bitwise_and)
+    cp(C_(P_), V("pi", 0, 1))
+    cp(C_(R_), V("pi", 1, 2))
+    ts(C_(Z8C), C_(P_), 16.0, A.mult, 15.0, A.add)
+    ts(V("mc"), V("jj", 0, 16), C_(R_), A.is_equal)
+    ts(V("z8"), V("jj", 0, 144, p=(0, 8)), C_(Z8C, (0, 8)), A.is_equal, 1024.0, A.mult)
+    ts(V("bc"), V("mc"), LOW, A.mult, -LOW, A.add)
+    ts(V("et"), V("mc"), LOW, A.mult)
+    tt(C_(G16), C_(P_), C_(R_), A.subtract)
+    ts(C_(WT), C_(R_), 2048.0, A.mult, 1024.0, A.add)
+    ts(C_(WT3), C_(R_), 6144.0, A.mult, 3072.0, A.add)
+    ts(C_(ZC), C_(G16), 15.0, A.add)
+    ts(C_(GA), C_(G16), -64.0, A.mult, 8192.0, A.add)
+    ts(V("zs"), V("jj", 0, 144), C_(ZC), A.is_equal)
+    diag, grp = [[-1, 128]], [[16, 8], [0, 16]]
+    ID = V("id1", 0, 128)
+    sel(V("id1"), V("rst", 0, 256), [[0, 2], [-1, 128]], A.is_equal, 0.0, 0, 1)
+    sel(V("bo"), V("rst", 0, 128), [[-16, 8], [0, 16]], A.is_ge, 0.0, 0, 1)
+    sel(V("bo"), V("bo"), grp, A.is_ge, 0.0, 15, -1)
+    sel(V("lo"), V("lo"), grp, A.is_ge, 0.0, 15, -1)
+    sel(V("lo"), V("lo"), diag, A.is_gt, 0.0, 0, 1)
+    sel(V("lo"), V("lo"), diag, A.not_equal, -1024.0, 0, 1)
+
+    def tblock(d):
+        act(V("tm", d * TW, (d + 1) * TW), V("jj", 0, TW), scale=V("mc", d, d + 1), bias=V("bc", d, d + 1))
+
+    def lists(out, z, src, start=True, stop=True):
+        return [(V(out, 0, 64), V(z, 15 - r, 143 - r), V(src, r, F, 16), start and r == 0, stop and r == 15) for r in range(16)]
+
+    def half(name, h, base=0):
+        return V(name, base + 512 * h, base + 512 * h + 512)
+
+    def quad(name, h):
+        return V(name, 256 * h, 256 * h + 256)
+
+    def offs(name, base, i, n):
+        w = 64 // n
+        return V(name, base + w * i, base + w * i + w)
+
+    def key_lists():
+        for i in range(2):
+            ts(V("kb", 64 * i, 64 * i + 64), V("wki"), 2 + 4 * i, A.logical_shift_right, 15 * TW, A.bitwise_and)
+        tt(V("kf"), V("kb"), V("fm"), A.add)
+        cp(V("ko"), V("kf"))
+
+    def far_lists(t, fa, out):
+        C = B0 + t * F
+        P = 1 << (C - 1).bit_length()
+        tt(V("hv", 0, 64), V("psL", 0, 64), V(fa), A.add)
+        cp(V("hv", 64, 128), V("psL", 0, 64))
+        ts(V("hv", 128, 192), V("hv", 0, 64), 10, A.logical_shift_right, 7, A.bitwise_and)
+        for q in range(N):
+            ts(V("oh", 64 * q, 64 * q + 64), V("hv", 128, 192), float(q), A.is_equal)
+        mm([(V("psX%d" % h, 0, 256), V("lo"), quad("oh", h), True, False) for h in range(2)])
+        run("v", V("sc"), [V("rst"), V("oh")], lambda: g.vector.tensor_tensor_scan(T.sc[:], T.rst[:], T.oh[:], 0.0, A.mult, A.add))
+        for h in range(2):
+            mm([(V("psX%d" % h, 0, 256), V("bo"), quad("sc", h), False, True)])
+        ts(V("hv", 192, 256), V("hv", 64, 128), 10, A.logical_shift_right, P - 1, A.bitwise_and)
+        ts(V("of", 64, 128), V("hv", 128, 192), float(CM), A.mult, float(Z0), A.add)
+        ts(quad("cm", 0), V("psX0", 0, 256), float(CAP - 1023), A.is_lt, 0.5, A.add)
+        act(quad("cm", 1), V("psX1", 0, 256), scale=-1.0, bias=CAP - 1023.5, func=AF.Sign)
+        mm([(V("psO", 0, 64), V("idh") if q >= 4 else ID, V("cm", 64 * q, 64 * q + 64), q == 0, q == N - 1) for q in range(N)])
+        ts(V("of", 0, 64), V("hv", 192, 256), float(C), A.is_ge, float(-C), A.mult)
+        tt(V("of", 128, 192), V("of", 64, 128), V("hv", 192, 256), A.add)
+        tt(V("of", 192, 256), V("of", 128, 192), V("of", 0, 64), A.add)
+        tt(V("of", 256, 320), V("psO", 0, 64), V("of", 192, 256), A.mult)
+        cp(out, V("of", 256, 320))
+
+    KY, RN = R0 + I0, R0 + I0 + 64
+    cp(V("hxb"), V("hx"))
+    mm(lists("psK", "z8", "hxb"))
+    cp(V("m1", RN, RN + 64), V("hn"))
+    cp(V("rt"), V("hr"))
+    for d in range(0, 4):
+        tblock(d)
+    for h in range(2):
+        act(half("p1", h), G(V("rt"), offs("m1", RN, h, 2)))
+    cp(V("wki"), V("psK", 0, 64))
+    ts(V("m1", KY, KY + 64), V("psK", 0, 64), 1.0 / 1024.0, A.mult)
+    ts(V("sb", 0, 64), V("wki"), 10, A.logical_shift_right, 15, A.bitwise_and)
+    ts(V("sb", 64, 128), V("wki"), 14, A.logical_shift_right, 15, A.bitwise_and)
+    cp(V("kd"), V("sb"))
+    cp(V("m1", 0, R0), V("hr"))
+    for h in range(2):
+        act(half("p2", h), G(V("et"), offs("kd", 64, h, 2)))
+    for h in range(2):
+        tt(half("mk", h), G(V("et"), offs("kd", 0, h, 2)), half("p1", h), A.min)
+    mm(lists("psL", "zs", "mk"))
+    cp(V("m1", R0, R0 + I0), V("hi"))
+    stage("m", "m1")
+    cp(V("m2", 128, 192), V("psL", 0, 64))
+    for d in range(4, 10):
+        tblock(d)
+    for h in range(2):
+        tt(half("mk", h), G(V("hi"), offs("m2", 128, h, 2)), half("p2", h), A.min)
+    mm(lists("psL", "zs", "mk"))
+    ts(V("zw"), V("jj", 0, 144), C_(ZC), A.is_equal, C_(WT), A.mult)
+    ts(V("fl", 0, 64), V("jj", 0, 64), 16.0, A.mult, C_(R_), A.add)
+    ts(V("fah"), V("fl", 0, 64), float(N - rank), A.add, 1024.0, A.mult)
+    cp(V("m2", 64, 128), V("psL", 0, 64))
+    cp(half("old", 0), G(V("hb"), offs("m2", 64, 0, 2)))
+    act(half("old", 1), G(V("hb"), offs("m2", 64, 1, 2)))
+    mm(lists("psL", "zw", "old"))
+    ms(V("rst", 0, 512, 64), 0.0)
+    ts(V("idh"), ID, 0.5, A.mult)
+    for d in range(10, 16):
+        tblock(d)
+    far_lists(0, "fah", V("m2", 0, 64))
+    stage("k", "m2")
+    iota(V("fm"), [[0, 8], [16, 16]])
+    for h in range(2):
+        iota(V("cq", 64 * h, 64 * h + 64), [[-15 * TW * (h + 1), 4], [0, 16]])
+    iota(V("jj", TW, F), [[1, F - TW]], TW)
+
+    def fill_far(lo, w, src, ks):
+        items = []
+        for k in ks:
+            c0 = Z0 + k * CM + lo
+            items.append(("y", V("ft", c0, c0 + w, p=(0, 128 - 16 * k)), src(k, N)))
+            if k:
+                items.append(("y", V("ft", c0, c0 + w, p=(128 - 16 * k, 128)), src(0, k)))
+        if items:
+            dma(items)
+
+    rest = [k for k in range(1, N) if k not in PE_SLOTS]
+    landed = lambda a, b: D("l_b", a, b)
+    fill_far(0, B0, landed, [0])
+    fill_far(0, B0, landed, rest[:PRE])
+    dma([("y", V("n1"), D("l_m"))])
+    fill_far(0, B0, landed, rest[PRE:])
+    dma([("y", V("n2"), D("l_k"))])
+    ts(V("zw3"), V("jj", 0, 144), C_(ZC), A.is_equal, C_(WT3), A.mult)
+    ts(V("id3"), ID, 3.0, A.mult)
+    ts(V("fao"), V("fl", 0, 64), 1024.0, A.mult, C_(GA), A.add)
+    ts(V("fm"), V("fm"), C_(R_), A.add)
+    banks = ("psA0", "psX0", "psA1", "psX1")
+    n = 0
+    for k in PE_SLOTS:
+        for j in range(B0 // 512):
+            bank = V(banks[n % 4])
+            mm([(bank, V("id1", 16 * k, 16 * k + 128), half("ft", j, Z0), True, True)])
+            (act if n % 2 else cp)(half("ft", j, Z0 + k * CM), bank)
+            n += 1
+
+    SCALE = (1.0, 1.0, 2.0, 2.0)
+    BIAS = (0.0, 1024.0, 2048.0, 4096.0)
+    RC = ("rt", "rca", "rcb", "rca")
+    todo = []
+
+    def fill(n):
+        for _ in range(n):
+            if todo:
+                todo.pop(0)()
+
+    def masks_of(name, t, base):
+        for i in range(4):
+            act(quad(name, i), G(V("tm"), offs("ko", base, i, 4)), scale=SCALE[t], bias=BIAS[t] + SCALE[t] * TW * i)
+
+    def it_window(t):
+        return V("it", 0, I0 + 4096 if t == 3 else I0 + t * F)
+
+    def root_append(t, off, base):
+        for i in range(4):
+            todo.append(lambda i=i: tt(quad(RC[t + 1], i), G(V(RC[t]), offs(off, base, i, 4)), quad("p1", i), A.max))
+
+    def inner_append(t, off, base):
+        for i in range(4):
+            if t < 2:
+                o = V("it", I0 + t * F + 256 * i, I0 + t * F + 256 * i + 256)
+            elif t == 2:
+                o = V("it", I0 + 2048 + 512 * i, I0 + 2048 + 512 * i + 512, 2)
+            else:
+                o = quad("rcb", i)
+            todo.append(lambda i=i, o=o: tt(o, G(it_window(t), offs(off, base, i, 4)), quad("p2", i), A.max))
+
+    def old_sums():
+        mm([(V("psA%d" % h), ID, half("old", h), True, False) for h in range(2)] + lists("psK", "zw", "old", stop=False))
+
+    def turn_mm(t, i):
+        if i < len(TURN):
+            for h, bank in enumerate(("psQ", "psO")):
+                mm([(V(bank), V("id1", 16 * TURN[i], 16 * TURN[i] + 128), half("ft", h, Z0 + B0 + (t - 1) * F), True, True)])
+
+    def turn_out(t, i):
+        if i < len(TURN):
+            for h, bank in enumerate(("psQ", "psO")):
+                act(half("ft", h, Z0 + TURN[i] * CM + B0 + (t - 1) * F), V(bank))
+
+    def picked(t):
+        s = 64 if SCALE[t] > 1 else 0
+        mm([(V("psL", 0, 64), ID, V("cq", s, s + 64), True, False)])
+        mm(lists("psL", "zs", "mk", start=False))
+
+    def finish(t, off):
+        last = t == RO - 1
+        C = B0 + t * F
+        mm([(V("psX%d" % h), ID, half("old", h), True, False) for h in range(2)])
+        cp(half("far", 0), G(V("ft"), offs(off, 0, 0, 2)))
+        act(half("far", 1), G(V("ft"), offs(off, 0, 1, 2)))
+        for h in range(2):
+            mm([(V("psA%d" % h), V("id3"), half("far", h), False, True)])
+        far3 = [(V("psX%d" % h), V("id3"), half("far", h), False, False) for h in range(2)]
+        carry = [(V("psX%d" % h), ID, half("qn", h), False, True) for h in range(2)]
+        mm(far3 if last else lists("psK", "zw3", "far", start=False))
+        fill(1)
+        qb = -(QB - 127.5 + t)
+        ts(half("qn", 0), V("psA0"), -1.0, A.mult, qb, A.add)
+        act(half("qn", 1), V("psA1"), scale=-1.0, bias=qb)
+        if last:
+            for h in range(2):
+                mm([carry[h]])
+            mm(lists("psK", "zw3", "far", start=False))
+            mm(lists("psQ", "zw", "qn"))
+            ts(half("yb_", 0), V("psX0"), QB + t, A.add)
+            act(half("yb_", 1), V("psX1"), bias=QB + t)
+            stage("y", "yb_")
+        else:
+            mm(lists("psQ", "zw", "qn"))
+            for h in range(2):
+                mm([far3[h], carry[h]])
+            cp(V("wki"), V("psK", 0, 64))
+        act(V("wkf"), V("psK", 0, 64), bias=1024.0 * 256.0 * (QB + t))
+        if not last:
+            key_lists()
+        tt(V("wj"), V("psQ", 0, 64), V("wkf"), A.add)
+        ts(V("sb", 0, 64), V("wj"), 13, A.logical_shift_right, F - 1, A.bitwise_and)
+        ts(V("sb", 64, 128), V("wj"), 7 * 1024, A.bitwise_and)
+        tt(V("sa", 0, 64), V("sb", 0, 64), V("sb", 64, 128), A.subtract)
+        tt(V("sa", 64, 128), V("sb", 64, 128), V("fl", 0, 64), A.min)
+        tt(V("sa", 128, 192), V("sa", 0, 64), V("sa", 64, 128), A.max)
+        cp(V("so"), V("sa", 128, 192))
+        fill(8)
+        if not last:
+            masks_of("p1", t + 1, 0)
+            for h in range(2):
+                act(half("ft", h, Z0 + C), V("psX%d" % h), bias=QB + t)
+            fill_far(C, F, lambda a, b: V("ft", Z0 + C, Z0 + C + F, p=(16 * a, 16 * b)), [k for k in range(1, N) if k not in TURN])
+            masks_of("p2", t + 1, 64)
+
+    ts(V("wki"), V("n1", KY, KY + 64), 1024.0, A.mult)
+    key_lists()
+    masks_of("p1", 0, 0)
+    ts(V("rt"), V("n1", 0, R0), float(-I0), A.add)
+    ts(V("it", 0, I0), V("n1", R0, R0 + I0), float(-B0), A.add)
+    masks_of("p2", 0, 64)
+    root_append(0, "n1", RN)
+    inner_append(0, "n2", 128)
+    fill(4)
+    cp(half("old", 0), G(V("ft", Z0, Z0 + B0), offs("n2", 64, 0, 2)))
+    act(half("old", 1), G(V("ft", Z0, Z0 + B0), offs("n2", 64, 1, 2)))
+    old_sums()
+    fill(3)
+    finish(0, "n2")
+
+    for t in range(1, RO):
+        low = 15.0 * (LOW * SCALE[t] - BIAS[t])
+        last = t == RO - 1
+        for h in range(2):
+            tt(half("mk", h), G(V(RC[t]), offs("so", 0, h, 2)), half("p1", h), A.min)
+        picked(t)
+        turn_mm(t, 0)
+        turn_out(t, 0)
+        if not last:
+            root_append(t, "so", 0)
+        fill(1)
+        ts(V("io_"), V("psL", 0, 64), low + I0, A.add)
+        for h in range(2):
+            tt(half("mk", h), G(it_window(t), offs("io_", 0, h, 2)), half("p2", h), A.min)
+        picked(t)
+        turn_mm(t, 1)
+        inner_append(t, "io_", 0)
+        fill(1)
+        if not last:
+            ts(V("bo_"), V("psL", 0, 64), low + B0, A.add)
+        else:
+            ts(V("sa", 0, 64), V("psL", 0, 64), low + B0, A.add)
+            ts(V("sa", 64, 128), V("psL", 0, 64), low + 5120.0, A.add, 0.5, A.mult)
+            tt(V("sa", 128, 192), V("sa", 0, 64), V("sa", 64, 128), A.min)
+            cp(V("bo_"), V("sa", 128, 192))
+        for h in range(2):
+            act(half("old", h), G(V("ft", Z0, Z0 + B0 + t * F), offs("bo_", 0, h, 2)))
+        turn_out(t, 1)
+        fill(5)
+        mm(lists("psL", "zw", "old"))
+        old_sums()
+        if last:
+            ts(V("yu"), V("rcb"), float(B0), A.add)
+            stage("i", "yu")
+        far_lists(t, "fao", V("fo"))
+        finish(t, "fo")
+
+    base = float(R0 + 3 * F)
+    ts(half("p1", 0), G(V("jj"), offs("so", 0, 0, 2)), base, A.add)
+    act(half("p1", 1), G(V("jj"), offs("so", 0, 1, 2)), bias=base)
+    stage("n", "p1", rows=(0, 128, 16))
+    dma([("y", V("yu"), D("l_i"))])
+    for h in range(2):
+        cp(half("p2", h), half("yu", h))
+        act(V("psA%d" % h), half("p2", h), scale=0.5, bias=1792.0)
+    for h in range(2):
+        tt(half("rca", h), half("p2", h), V("psA%d" % h), A.min)
+        dma([("y", X(T.yi[:, 512 * h:512 * h + 512]), half("rca", h))])
+    dma([("s", X(T.yb[:]), D("l_y"))])
+    dma([("y", X(T.yn[:]), D("l_n"))])
+    totals.update(count)
+    for sem, val in totals.items():
+        need("g", (sem, val, {}))

@@ -6,38 +6,42 @@ AF = ActivationFunctionType
 N, R0, I0, B0, F, CAP, RO = 8, 256, 1152, 1536, 1024, 144, 4
 CM = B0 + 3 * F
 Z0 = 16
-W1 = R0 + I0 + 128
-W2 = 192
+RN, KY, WE = R0, R0 + 64, R0 + 128
+IO, BO, W1 = I0, I0 + 64, I0 + 128
 TW = 256
 LOW = 8192.0
 QB = 49152.0
-PE_SLOTS = (4, 5, 6, 7)
-TURN = (6, 7)
-PRE = 1
+FB = 192.0
+OK = 65536.0
+PE_SLOTS = (5, 6, 7)
+TURN = (4, 5, 6, 7)
+DIAG = (-512.0, -1536.0, -2560.0, -3584.0, -4608.0, OK, OK / 2, 3.0)
 
 SB = lambda n, d="float32", p=128: ("sbuf", [p, n], d)
 BF, I32, U16 = "bfloat16", "int32", "uint16"
 SCRATCH = {
-    "ft": SB(Z0 + 8 * CM, BF), "tm": SB(16 * TW), "it": SB(I0 + 4096), "rt": SB(R0), "rca": SB(F), "rcb": SB(F),
+    "ft": SB(Z0 + 8 * CM, BF), "tm": SB(16 * TW), "it": SB(I0 + 4096), "rt": SB(R0), "rh": SB(R0), "rca": SB(F), "rcb": SB(F),
     "p1": SB(F), "p2": SB(F), "mk": SB(F, "float16"), "old": SB(F, BF), "far": SB(F, BF), "qn": SB(F, BF),
     "hr": SB(R0, I32), "hi": SB(I0, I32), "hn": SB(64, I32), "hb": SB(B0, BF), "hx": SB(F, I32, 8), "hxb": SB(F, BF, 8),
-    "m1": SB(W1, U16), "m2": SB(W2, U16), "n1": SB(W1, U16), "n2": SB(W2, U16),
-    "jj": SB(F), "pi": SB(8, I32), "col": SB(16),
+    "e1": SB(WE, U16), "e2": SB(WE, U16), "m1": SB(W1, U16), "m2": SB(64, U16), "n1": SB(W1, U16), "n2": SB(64, U16),
+    "jj": SB(TW), "pi": SB(8, I32), "col": SB(16),
     "zw": SB(144, BF), "zw3": SB(144, BF), "zs": SB(144, "float16"), "z8": SB(144, BF, 8),
-    "id1": SB(256, BF), "id3": SB(128, BF), "idh": SB(128, BF), "bo": SB(128, BF), "lo": SB(128, BF),
-    "rst": SB(512, BF), "fl": SB(64), "fm": SB(128), "fah": SB(64), "fao": SB(64), "et": SB(16), "mc": SB(16), "bc": SB(16),
+    "id1": SB(256, BF), "idf": SB(128), "dg": SB(128 * len(DIAG), BF), "bo": SB(128, BF), "lo": SB(128, BF),
+    "rst": SB(512, BF), "fl": SB(64), "fn": SB(64), "fm": SB(128), "fah": SB(64), "fao": SB(64),
+    "et": SB(16), "mc": SB(16), "bc": SB(16),
     "cq": SB(128, BF), "oh": SB(512, BF), "sc": SB(512, BF), "cm": SB(512, BF),
     "wki": SB(64, I32), "wkf": SB(64), "kb": SB(128, I32), "kf": SB(128), "ko": SB(128, U16), "kd": SB(128, U16),
     "wj": SB(64, I32), "sb": SB(128, I32), "sa": SB(192), "so": SB(64, U16), "io_": SB(64, U16), "bo_": SB(64, U16),
-    "hv": SB(256, I32), "of": SB(320), "fo": SB(64, U16), "yu": SB(F, U16), "yb_": SB(F, BF),
+    "hv": SB(128, I32), "hf": SB(64), "hq": SB(192, BF), "fo": SB(64, U16), "yu": SB(F, U16), "yb_": SB(F, BF), "yn_": SB(64),
 }
-for _k in ("A0", "A1", "L", "K", "Q", "X0", "X1", "O"):
+for _k in ("A0", "A1", "L0", "L1", "K", "Q", "X0", "X1"):
     SCRATCH["ps" + _k] = ("psum", [128, 512], "float32")
-MSG = {"b": (B0 // 8, BF), "m": (W1 // 8, U16), "k": (W2 // 8, U16), "i": (F // 8, U16), "y": (F // 8, BF), "n": (F // 128, "float32")}
+MSG = {"b": (B0 // 8, BF), "e": (WE // 8, U16), "m": (W1 // 8, U16), "k": (8, U16),
+       "i": (F // 8, U16), "y": (F // 8, BF), "n": (F // 128, "float32")}
 for _k, (_n, _d) in MSG.items():
     SCRATCH["s_" + _k] = ("dram", [N, 128, _n], _d)
     SCRATCH["l_" + _k] = ("dram", [N, 128, _n], _d)
-SEMAPHORES = ["cv", "cs", "ct", "cg"] + ["d%d" % i for i in range(40)] + ["arr_" + k for k in MSG] + ["out_" + k for k in MSG]
+SEMAPHORES = ["cv", "cs", "ct", "cg"] + ["d%d" % i for i in range(70)] + ["arr_" + k for k in MSG] + ["out_" + k for k in MSG]
 
 
 def routes(T, topo):
@@ -188,8 +192,8 @@ def rank_program(g, core, T, topo):
     def sel(out, x, pattern, op, fill_, base, ch):
         run("g", out, [x], lambda: g.affine_select(out[0], x[0], pattern, op, fill_, base, ch))
 
-    def iota(out, pattern, base=0):
-        run("g", out, [], lambda: g.iota(out[0], pattern, base, 0, allow_small_or_imprecise_dtypes=True))
+    def iota(out, pattern, base=0, ch=0):
+        run("g", out, [], lambda: g.iota(out[0], pattern, base, ch, allow_small_or_imprecise_dtypes=True))
 
     def mm(items):
         rd = sorted(set(r for it in items for r in it[1][1] + it[2][1]))
@@ -241,26 +245,34 @@ def rank_program(g, core, T, topo):
                 note("far", [], [("l_" + k, a, a + 1)], ("arr_" + k, n_arr, {}))
     own = (16 * rank, 16 * rank + 16)
 
-    def stage(k, src, rows=None):
-        dma([("y", D("s_" + k), V(src, p=rows))])
-        dma([("y", D("l_" + k, rank, rank + 1), V(src, p=own if rows is None else (own[0], own[0] + 1)))])
+    def stage(k, src):
+        dma([("y", D("s_" + k), V(src))])
+        dma([("y", D("l_" + k, rank, rank + 1), V(src, p=own))])
         send(k)
 
     dma([("s", V("hx"), X(T.x0[:]))])
-    dma([("y", V("hn"), X(T.rn0[:])), ("s", V("hr"), X(T.rtab[:]))])
+    dma([("y", V("hr"), X(T.rtab[:])), ("s", V("hn"), X(T.rn0[:]))])
     dma([("y", D("s_b"), X(T.btab[:]))])
     dma([("y", V("hi"), X(T.itab[:]))])
     dma([("y", V("hb"), X(T.btab[:]))])
     dma([("y", D("l_b", rank, rank + 1), X(T.btab[own[0]:own[1], :]))])
 
     run("g", V("pi", 0, 1), [], lambda: g.iota(T.pi[:, 0:1], [[0, 1]], 0, 1))
-    iota(V("jj", 0, TW), [[1, TW]])
-    send("b")
+    iota(V("jj"), [[1, TW]])
     C_ = lambda i, p=None: V("col", i, i + 1, p=p)
-    P_, R_, G16, ZC, WT, WT3, Z8C, GA = range(8)
+    P_, R_, G16, ZC, WT, WT3, Z8C, GA, R64 = range(9)
     ms(V("rst"), 1.0)
     ms(V("lo"), -1.0)
     ms(V("ft", 0, Z0), 0.0)
+    diag, grp = [[-1, 128]], [[16, 8], [0, 16]]
+    ID = V("id1", 0, 128)
+    sel(V("id1"), V("rst", 0, 256), [[0, 2], [-1, 128]], A.is_equal, 0.0, 0, 1)
+    sel(V("bo"), V("rst", 0, 128), [[-16, 8], [0, 16]], A.is_ge, 0.0, 0, 1)
+    send("b")
+    sel(V("bo"), V("bo"), grp, A.is_ge, 0.0, 15, -1)
+    sel(V("lo"), V("lo"), grp, A.is_ge, 0.0, 15, -1)
+    sel(V("lo"), V("lo"), diag, A.is_gt, 0.0, 0, 1)
+    sel(V("lo"), V("lo"), diag, A.not_equal, -1024.0, 0, 1)
     ts(V("pi", 1, 2), V("pi", 0, 1), 15, A.bitwise_and)
     cp(C_(P_), V("pi", 0, 1))
     cp(C_(R_), V("pi", 1, 2))
@@ -271,24 +283,27 @@ def rank_program(g, core, T, topo):
     ts(V("et"), V("mc"), LOW, A.mult)
     tt(C_(G16), C_(P_), C_(R_), A.subtract)
     ts(C_(WT), C_(R_), 2048.0, A.mult, 1024.0, A.add)
-    ts(C_(WT3), C_(R_), 6144.0, A.mult, 3072.0, A.add)
     ts(C_(ZC), C_(G16), 15.0, A.add)
-    ts(C_(GA), C_(G16), -64.0, A.mult, 8192.0, A.add)
     ts(V("zs"), V("jj", 0, 144), C_(ZC), A.is_equal)
-    diag, grp = [[-1, 128]], [[16, 8], [0, 16]]
-    ID = V("id1", 0, 128)
-    sel(V("id1"), V("rst", 0, 256), [[0, 2], [-1, 128]], A.is_equal, 0.0, 0, 1)
-    sel(V("bo"), V("rst", 0, 128), [[-16, 8], [0, 16]], A.is_ge, 0.0, 0, 1)
-    sel(V("bo"), V("bo"), grp, A.is_ge, 0.0, 15, -1)
-    sel(V("lo"), V("lo"), grp, A.is_ge, 0.0, 15, -1)
-    sel(V("lo"), V("lo"), diag, A.is_gt, 0.0, 0, 1)
-    sel(V("lo"), V("lo"), diag, A.not_equal, -1024.0, 0, 1)
+    ts(V("zw"), V("jj", 0, 144), C_(ZC), A.is_equal, C_(WT), A.mult)
+    ts(V("fl"), V("jj", 0, 64), 16.0, A.mult, C_(R_), A.add)
+    ts(V("fah"), V("fl"), float(N - rank), A.add, 1024.0, A.mult)
+
+    def DG(c):
+        i = DIAG.index(float(c))
+        return V("dg", 128 * i, 128 * i + 128)
 
     def tblock(d):
-        act(V("tm", d * TW, (d + 1) * TW), V("jj", 0, TW), scale=V("mc", d, d + 1), bias=V("bc", d, d + 1))
+        act(V("tm", d * TW, (d + 1) * TW), V("jj"), scale=V("mc", d, d + 1), bias=V("bc", d, d + 1))
 
-    def lists(out, z, src, start=True, stop=True):
-        return [(V(out, 0, 64), V(z, 15 - r, 143 - r), V(src, r, F, 16), start and r == 0, stop and r == 15) for r in range(16)]
+    def lists(out, z, src, start=True, stop=True, h=None, at=None):
+        lo, w = (0, 64) if h is None else (32 * h, 32)
+        at = lo if at is None else at
+        return [(V(out, at, at + w), V(z, 15 - r, 143 - r), V(src, 16 * lo + r, 16 * (lo + w), 16), start and r == 0, stop and r == 15)
+                for r in range(16)]
+
+    def rows(out, z, src, start=True, stop=True):
+        return [(V(out, 0, 64), V(z, 15 - r, 143 - r), V(src, 64 * r, 64 * r + 64), start and r == 0, stop and r == 15) for r in range(16)]
 
     def half(name, h, base=0):
         return V(name, base + 512 * h, base + 512 * h + 512)
@@ -306,74 +321,125 @@ def rank_program(g, core, T, topo):
         tt(V("kf"), V("kb"), V("fm"), A.add)
         cp(V("ko"), V("kf"))
 
+    todo = []
+    turns = []
+
+    def fill(n):
+        for _ in range(n):
+            if todo:
+                todo.pop(0)()
+
+    def turn(n):
+        for _ in range(n):
+            if turns:
+                turns.pop(0)()
+
     def far_lists(t, fa, out):
         C = B0 + t * F
         P = 1 << (C - 1).bit_length()
-        tt(V("hv", 0, 64), V("psL", 0, 64), V(fa), A.add)
-        cp(V("hv", 64, 128), V("psL", 0, 64))
-        ts(V("hv", 128, 192), V("hv", 0, 64), 10, A.logical_shift_right, 7, A.bitwise_and)
+        H, S = V("psL0", 0, 64), V("psL1", 0, 64)
+        tt(V("hv", 0, 64), H, V(fa), A.add)
+        ts(V("hv", 64, 128), V("hv", 0, 64), 10, A.logical_shift_right, 7, A.bitwise_and)
+        act(V("hf"), H, scale=1.0 / 1024.0)
+        for i in range(2):
+            act(V("hq", 64 * i, 64 * i + 64), H, scale=1.0 / (1024.0 * P), bias=FB - 0.5 + 0.5 / P + i * (P - C) / P)
+        turn(1)
         for q in range(N):
-            ts(V("oh", 64 * q, 64 * q + 64), V("hv", 128, 192), float(q), A.is_equal)
+            ts(V("oh", 64 * q, 64 * q + 64), V("hv", 64, 128), float(q), A.is_equal)
         mm([(V("psX%d" % h, 0, 256), V("lo"), quad("oh", h), True, False) for h in range(2)])
         run("v", V("sc"), [V("rst"), V("oh")], lambda: g.vector.tensor_tensor_scan(T.sc[:], T.rst[:], T.oh[:], 0.0, A.mult, A.add))
         for h in range(2):
             mm([(V("psX%d" % h, 0, 256), V("bo"), quad("sc", h), False, True)])
-        ts(V("hv", 192, 256), V("hv", 64, 128), 10, A.logical_shift_right, P - 1, A.bitwise_and)
-        ts(V("of", 64, 128), V("hv", 128, 192), float(CM), A.mult, float(Z0), A.add)
+        ts(V("hq", 128, 192), V("hv", 64, 128), -1.0, A.mult)
+        mm([(S, V("idf"), V("hf"), True, False), (S, DG(C - P), V("hq", 0, 64), False, False), (S, DG(-C), V("hq", 64, 128), False, False),
+            (S, DG(-CM), V("hq", 128, 192), False, False)])
+        fill(1)
         ts(quad("cm", 0), V("psX0", 0, 256), float(CAP - 1023), A.is_lt, 0.5, A.add)
         act(quad("cm", 1), V("psX1", 0, 256), scale=-1.0, bias=CAP - 1023.5, func=AF.Sign)
-        mm([(V("psO", 0, 64), V("idh") if q >= 4 else ID, V("cm", 64 * q, 64 * q + 64), q == 0, q == N - 1) for q in range(N)])
-        ts(V("of", 0, 64), V("hv", 192, 256), float(C), A.is_ge, float(-C), A.mult)
-        tt(V("of", 128, 192), V("of", 64, 128), V("hv", 192, 256), A.add)
-        tt(V("of", 192, 256), V("of", 128, 192), V("of", 0, 64), A.add)
-        tt(V("of", 256, 320), V("psO", 0, 64), V("of", 192, 256), A.mult)
-        cp(out, V("of", 256, 320))
+        turn(1)
+        mm([(S, DG(OK / 2 if q >= 4 else OK), V("cm", 64 * q, 64 * q + 64), False, q == N - 1) for q in range(N)])
+        turn(8)
+        fill(1)
+        ts(out, S, Z0 - OK + FB * P, A.add)
 
-    KY, RN = R0 + I0, R0 + I0 + 64
-    cp(V("hxb"), V("hx"))
+    def walk(pick1, pick2, pre, conv1, conv2, old_win, bo):
+        for h in range(2):
+            pre(h)
+            pick1(h, 2)
+            mm(lists("psL%d" % h, "zs", "mk", start=pre is nothing, h=h, at=0))
+        conv1(0)
+        pre(0)
+        pick2(0, 2)
+        turn(1)
+        mm(lists("psL0", "zs", "mk", start=pre is nothing, h=0, at=0))
+        conv1(1)
+        pre(1)
+        pick2(2, 4)
+        conv2(0)
+        act(half("old", 0), G(old_win, offs(bo[0], bo[1], 0, 2)))
+        pick2(3, 4)
+        mm(lists("psL1", "zs", "mk", start=pre is nothing, h=1, at=0))
+        mm(lists("psL0", "zw", "old", h=0))
+        fill(1)
+        conv2(1)
+        cp(quad("old", 2), G(old_win, offs(bo[0], bo[1], 2, 4)))
+        act(quad("old", 3), G(old_win, offs(bo[0], bo[1], 3, 4)))
+        turn(1)
+        mm(lists("psL0", "zw", "old", h=1))
+        fill(1)
+
+    def nothing(h):
+        pass
+
+    def part(name, i, n):
+        w = F // n
+        return V(name, w * i, w * i + w)
+
+    cp(half("hxb", 0), half("hx", 0))
+    cp(V("e1", RN, RN + 64), V("hn"))
+    cp(V("rh"), V("hr"))
+    cp(half("hxb", 1), half("hx", 1))
     mm(lists("psK", "z8", "hxb"))
-    cp(V("m1", RN, RN + 64), V("hn"))
-    cp(V("rt"), V("hr"))
+    cp(V("e1", 0, R0), V("hr"))
     for d in range(0, 4):
         tblock(d)
     for h in range(2):
-        act(half("p1", h), G(V("rt"), offs("m1", RN, h, 2)))
+        act(half("p1", h), G(V("rh"), offs("e1", RN, h, 2)))
     cp(V("wki"), V("psK", 0, 64))
-    ts(V("m1", KY, KY + 64), V("psK", 0, 64), 1.0 / 1024.0, A.mult)
-    ts(V("sb", 0, 64), V("wki"), 10, A.logical_shift_right, 15, A.bitwise_and)
-    ts(V("sb", 64, 128), V("wki"), 14, A.logical_shift_right, 15, A.bitwise_and)
-    cp(V("kd"), V("sb"))
-    cp(V("m1", 0, R0), V("hr"))
-    for h in range(2):
-        act(half("p2", h), G(V("et"), offs("kd", 64, h, 2)))
-    for h in range(2):
-        tt(half("mk", h), G(V("et"), offs("kd", 0, h, 2)), half("p1", h), A.min)
-    mm(lists("psL", "zs", "mk"))
-    cp(V("m1", R0, R0 + I0), V("hi"))
-    stage("m", "m1")
-    cp(V("m2", 128, 192), V("psL", 0, 64))
-    for d in range(4, 10):
-        tblock(d)
-    for h in range(2):
-        tt(half("mk", h), G(V("hi"), offs("m2", 128, h, 2)), half("p2", h), A.min)
-    mm(lists("psL", "zs", "mk"))
-    ts(V("zw"), V("jj", 0, 144), C_(ZC), A.is_equal, C_(WT), A.mult)
-    ts(V("fl", 0, 64), V("jj", 0, 64), 16.0, A.mult, C_(R_), A.add)
-    ts(V("fah"), V("fl", 0, 64), float(N - rank), A.add, 1024.0, A.mult)
-    cp(V("m2", 64, 128), V("psL", 0, 64))
-    cp(half("old", 0), G(V("hb"), offs("m2", 64, 0, 2)))
-    act(half("old", 1), G(V("hb"), offs("m2", 64, 1, 2)))
-    mm(lists("psL", "zw", "old"))
-    ms(V("rst", 0, 512, 64), 0.0)
-    ts(V("idh"), ID, 0.5, A.mult)
-    for d in range(10, 16):
-        tblock(d)
-    far_lists(0, "fah", V("m2", 0, 64))
-    stage("k", "m2")
+    ts(V("e1", KY, KY + 64), V("psK", 0, 64), 1.0 / 1024.0, A.mult)
+    stage("e", "e1")
     iota(V("fm"), [[0, 8], [16, 16]])
     for h in range(2):
         iota(V("cq", 64 * h, 64 * h + 64), [[-15 * TW * (h + 1), 4], [0, 16]])
-    iota(V("jj", TW, F), [[1, F - TW]], TW)
+    ts(V("sb", 0, 64), V("wki"), 10, A.logical_shift_right, 15, A.bitwise_and)
+    ts(V("sb", 64, 128), V("wki"), 14, A.logical_shift_right, 15, A.bitwise_and)
+    cp(V("kd"), V("sb"))
+    for h in range(2):
+        act(half("p2", h), G(V("et"), offs("kd", 64, h, 2)))
+    for d in range(4, 7):
+        tblock(d)
+
+    def home_consts():
+        cp(V("idf"), ID)
+        for c in (-512, -1536, -CM, OK, OK / 2):
+            ts(DG(c), ID, float(c), A.mult)
+
+    for h in range(2):
+        todo.append(lambda h=h: cp(V("m1", h * I0 // 2, (h + 1) * I0 // 2), V("hi", h * I0 // 2, (h + 1) * I0 // 2)))
+    todo.append(home_consts)
+    walk(lambda i, n: tt(part("mk", i, n), G(V("et"), offs("kd", 0, i, n)), part("p1", i, n), A.min),
+         lambda i, n: tt(part("mk", i, n), G(V("hi"), offs("m1", IO, i, n)), part("p2", i, n), A.min),
+         nothing,
+         lambda h: cp(offs("m1", IO, h, 2), V("psL%d" % h, 0, 32)),
+         lambda h: cp(offs("m1", BO, h, 2), V("psL%d" % h, 0, 32)),
+         V("hb"), ("m1", BO))
+    stage("m", "m1")
+    fill(1)
+    ms(V("rst", 0, 512, 64), 0.0)
+    far_lists(0, "fah", V("m2"))
+    stage("k", "m2")
+    for d in range(7, 16):
+        tblock(d)
 
     def fill_far(lo, w, src, ks):
         items = []
@@ -388,36 +454,28 @@ def rank_program(g, core, T, topo):
     rest = [k for k in range(1, N) if k not in PE_SLOTS]
     landed = lambda a, b: D("l_b", a, b)
     fill_far(0, B0, landed, [0])
-    fill_far(0, B0, landed, rest[:PRE])
+    dma([("y", V("e2"), D("l_e"))])
+    fill_far(0, B0, landed, rest[:2])
     dma([("y", V("n1"), D("l_m"))])
-    fill_far(0, B0, landed, rest[PRE:])
+    fill_far(0, B0, landed, rest[2:])
     dma([("y", V("n2"), D("l_k"))])
+    ts(C_(WT3), C_(R_), 6144.0, A.mult, 3072.0, A.add)
+    ts(C_(GA), C_(G16), -64.0, A.mult, 8192.0, A.add)
+    ts(C_(R64), C_(R_), 64.0, A.mult)
     ts(V("zw3"), V("jj", 0, 144), C_(ZC), A.is_equal, C_(WT3), A.mult)
-    ts(V("id3"), ID, 3.0, A.mult)
-    ts(V("fao"), V("fl", 0, 64), 1024.0, A.mult, C_(GA), A.add)
+    for c in (3, -2560, -3584):
+        ts(DG(c), ID, float(c), A.mult)
+    ts(V("fao"), V("fl"), 1024.0, A.mult, C_(GA), A.add)
+    ts(V("fn"), V("jj", 0, 64), C_(R64), A.add)
     ts(V("fm"), V("fm"), C_(R_), A.add)
-    banks = ("psA0", "psX0", "psA1", "psX1")
-    n = 0
-    for k in PE_SLOTS:
-        for j in range(B0 // 512):
-            bank = V(banks[n % 4])
-            mm([(bank, V("id1", 16 * k, 16 * k + 128), half("ft", j, Z0), True, True)])
-            (act if n % 2 else cp)(half("ft", j, Z0 + k * CM), bank)
-            n += 1
 
     SCALE = (1.0, 1.0, 2.0, 2.0)
     BIAS = (0.0, 1024.0, 2048.0, 4096.0)
     RC = ("rt", "rca", "rcb", "rca")
-    todo = []
 
-    def fill(n):
-        for _ in range(n):
-            if todo:
-                todo.pop(0)()
-
-    def masks_of(name, t, base):
-        for i in range(4):
-            act(quad(name, i), G(V("tm"), offs("ko", base, i, 4)), scale=SCALE[t], bias=BIAS[t] + SCALE[t] * TW * i)
+    def mask_q(name, t, i):
+        base = 0 if name == "p1" else 64
+        act(quad(name, i), G(V("tm"), offs("ko", base, i, 4)), scale=SCALE[t], bias=BIAS[t] + SCALE[t] * TW * i)
 
     def it_window(t):
         return V("it", 0, I0 + 4096 if t == 3 else I0 + t * F)
@@ -436,135 +494,149 @@ def rank_program(g, core, T, topo):
                 o = quad("rcb", i)
             todo.append(lambda i=i, o=o: tt(o, G(it_window(t), offs(off, base, i, 4)), quad("p2", i), A.max))
 
-    def old_sums():
-        mm([(V("psA%d" % h), ID, half("old", h), True, False) for h in range(2)] + lists("psK", "zw", "old", stop=False))
-
-    def turn_mm(t, i):
-        if i < len(TURN):
-            for h, bank in enumerate(("psQ", "psO")):
-                mm([(V(bank), V("id1", 16 * TURN[i], 16 * TURN[i] + 128), half("ft", h, Z0 + B0 + (t - 1) * F), True, True)])
-
-    def turn_out(t, i):
-        if i < len(TURN):
-            for h, bank in enumerate(("psQ", "psO")):
-                act(half("ft", h, Z0 + TURN[i] * CM + B0 + (t - 1) * F), V(bank))
-
-    def picked(t):
-        s = 64 if SCALE[t] > 1 else 0
-        mm([(V("psL", 0, 64), ID, V("cq", s, s + 64), True, False)])
-        mm(lists("psL", "zs", "mk", start=False))
+    def turned(k, c0, bank, copy):
+        mm([(V(bank), V("id1", 16 * k, 16 * k + 128), V("ft", Z0 + c0, Z0 + c0 + 512), True, True)])
+        copy(V("ft", Z0 + k * CM + c0, Z0 + k * CM + c0 + 512), V(bank))
 
     def finish(t, off):
         last = t == RO - 1
         C = B0 + t * F
-        mm([(V("psX%d" % h), ID, half("old", h), True, False) for h in range(2)])
+        base = lambda b, h: (V("ps%s%d" % (b, h)), ID, half("old", h), True, False)
+        far3 = lambda b, h, stop: (V("ps%s%d" % (b, h)), DG(3), half("far", h), False, stop)
+        carry = lambda h: (V("psX%d" % h), ID, half("qn", h), False, True)
+        mm([base("A", h) for h in range(2)])
         cp(half("far", 0), G(V("ft"), offs(off, 0, 0, 2)))
         act(half("far", 1), G(V("ft"), offs(off, 0, 1, 2)))
+        mm([base("X", h) for h in range(2)] if last else lists("psK", "zw", "old", stop=False))
         for h in range(2):
-            mm([(V("psA%d" % h), V("id3"), half("far", h), False, True)])
-        far3 = [(V("psX%d" % h), V("id3"), half("far", h), False, False) for h in range(2)]
-        carry = [(V("psX%d" % h), ID, half("qn", h), False, True) for h in range(2)]
-        mm(far3 if last else lists("psK", "zw3", "far", start=False))
+            mm([far3("A", h, True)])
+        mm([far3("X", h, False) for h in range(2)] if last else lists("psK", "zw3", "far", start=False))
         fill(1)
         qb = -(QB - 127.5 + t)
         ts(half("qn", 0), V("psA0"), -1.0, A.mult, qb, A.add)
         act(half("qn", 1), V("psA1"), scale=-1.0, bias=qb)
         if last:
             for h in range(2):
-                mm([carry[h]])
-            mm(lists("psK", "zw3", "far", start=False))
-            mm(lists("psQ", "zw", "qn"))
+                mm([carry(h)])
             ts(half("yb_", 0), V("psX0"), QB + t, A.add)
             act(half("yb_", 1), V("psX1"), bias=QB + t)
             stage("y", "yb_")
+            mm(rows("psQ", "zw", "yb_"))
+            cp(V("wj"), V("psQ", 0, 64))
         else:
             mm(lists("psQ", "zw", "qn"))
             for h in range(2):
-                mm([far3[h], carry[h]])
+                mm([base("X", h), far3("X", h, False), carry(h)])
             cp(V("wki"), V("psK", 0, 64))
-        act(V("wkf"), V("psK", 0, 64), bias=1024.0 * 256.0 * (QB + t))
-        if not last:
+            act(V("wkf"), V("psK", 0, 64), bias=1024.0 * 256.0 * (QB + t))
             key_lists()
-        tt(V("wj"), V("psQ", 0, 64), V("wkf"), A.add)
+            tt(V("wj"), V("psQ", 0, 64), V("wkf"), A.add)
         ts(V("sb", 0, 64), V("wj"), 13, A.logical_shift_right, F - 1, A.bitwise_and)
         ts(V("sb", 64, 128), V("wj"), 7 * 1024, A.bitwise_and)
         tt(V("sa", 0, 64), V("sb", 0, 64), V("sb", 64, 128), A.subtract)
-        tt(V("sa", 64, 128), V("sb", 64, 128), V("fl", 0, 64), A.min)
+        tt(V("sa", 64, 128), V("sb", 64, 128), V("fn" if last else "fl"), A.min)
         tt(V("sa", 128, 192), V("sa", 0, 64), V("sa", 64, 128), A.max)
-        cp(V("so"), V("sa", 128, 192))
+        if last:
+            ts(V("yn_"), V("sa", 128, 192), float(R0 + t * F), A.add)
+            stage("n", "yn_")
+            return
         fill(8)
-        if not last:
-            masks_of("p1", t + 1, 0)
-            for h in range(2):
-                act(half("ft", h, Z0 + C), V("psX%d" % h), bias=QB + t)
-            fill_far(C, F, lambda a, b: V("ft", Z0 + C, Z0 + C + F, p=(16 * a, 16 * b)), [k for k in range(1, N) if k not in TURN])
-            masks_of("p2", t + 1, 64)
+        cp(V("so"), V("sa", 128, 192))
 
-    ts(V("wki"), V("n1", KY, KY + 64), 1024.0, A.mult)
+        def new_half(h):
+            c0 = C + 512 * h
+            act(V("ft", Z0 + c0, Z0 + c0 + 512), V("psX%d" % h), bias=QB + t)
+            fill_far(c0, 512, lambda a, b: V("ft", Z0 + c0, Z0 + c0 + 512, p=(16 * a, 16 * b)),
+                     [k for k in range(1, N) if h == 0 or k not in TURN])
+
+        for i in range(2):
+            mask_q("p1", t + 1, i)
+        new_half(0)
+        for i in range(2, 4):
+            mask_q("p1", t + 1, i)
+        for i in range(4):
+            mask_q("p2", t + 1, i)
+        new_half(1)
+        for i, k in enumerate(TURN):
+            turns.append(lambda i=i, k=k: turned(k, C + 512, ("psQ", "psK")[i % 2], act))
+
+    ts(V("wki"), V("e2", KY, KY + 64), 1024.0, A.mult)
     key_lists()
-    masks_of("p1", 0, 0)
-    ts(V("rt"), V("n1", 0, R0), float(-I0), A.add)
-    ts(V("it", 0, I0), V("n1", R0, R0 + I0), float(-B0), A.add)
-    masks_of("p2", 0, 64)
-    root_append(0, "n1", RN)
-    inner_append(0, "n2", 128)
-    fill(4)
-    cp(half("old", 0), G(V("ft", Z0, Z0 + B0), offs("n2", 64, 0, 2)))
-    act(half("old", 1), G(V("ft", Z0, Z0 + B0), offs("n2", 64, 1, 2)))
-    old_sums()
-    fill(3)
+    for name in ("p1", "p2"):
+        for i in range(4):
+            mask_q(name, 0, i)
+    banks = ("psA0", "psX0", "psA1", "psX1")
+    n, NA, NV = 0, 3, 6
+    for k in PE_SLOTS:
+        for j in range(B0 // 512):
+            turned(k, 512 * j, banks[n % 4], act if n >= NV else cp)
+            n += 1
+            if n == NA:
+                ts(V("rt"), V("e2", 0, R0), float(-I0), A.add)
+                root_append(0, "e2", RN)
+                fill(4)
+    act(half("old", 0), G(V("ft", Z0, Z0 + B0), offs("n1", BO, 0, 2)))
+    act(half("old", 1), G(V("ft", Z0, Z0 + B0), offs("n1", BO, 1, 2)))
+    ts(V("it", 0, I0), V("n1", 0, I0), float(-B0), A.add)
+    inner_append(0, "n1", IO)
+    fill(1)
     finish(0, "n2")
+
+    def inner_out(h):
+        ts(half("yu", h), half("rcb", h), float(B0), A.add)
+        dma([("y", (T.s_i[:, 64 * h:64 * h + 64, :], [("s_i", 4 * h, 4 * h + 4)]), half("yu", h)),
+             ("y", (T.l_i[rank, 64 * h:64 * h + 64, :], [("l_i", N + h, N + h + 1)]), V("yu", 512 * h, 512 * h + 512, p=own))])
+        if h:
+            send("i")
 
     for t in range(1, RO):
         low = 15.0 * (LOW * SCALE[t] - BIAS[t])
         last = t == RO - 1
-        for h in range(2):
-            tt(half("mk", h), G(V(RC[t]), offs("so", 0, h, 2)), half("p1", h), A.min)
-        picked(t)
-        turn_mm(t, 0)
-        turn_out(t, 0)
+        s0 = 64 if SCALE[t] > 1 else 0
+
+        def pre(h):
+            mm([(V("psL%d" % h, 0, 32), ID, V("cq", s0 + 32 * h, s0 + 32 * h + 32), True, False)])
+
+        def conv2(h):
+            L = V("psL%d" % h, 0, 32)
+            if not last:
+                ts(offs("bo_", 0, h, 2), L, low + B0, A.add)
+            else:
+                ts(V("sa", 0, 32), L, low + B0, A.add)
+                ts(V("sa", 64, 96), L, low + 5120.0, A.add, 0.5, A.mult)
+                tt(V("sa", 128, 160), V("sa", 0, 32), V("sa", 64, 96), A.min)
+                cp(offs("bo_", 0, h, 2), V("sa", 128, 160))
+
         if not last:
             root_append(t, "so", 0)
-        fill(1)
-        ts(V("io_"), V("psL", 0, 64), low + I0, A.add)
-        for h in range(2):
-            tt(half("mk", h), G(it_window(t), offs("io_", 0, h, 2)), half("p2", h), A.min)
-        picked(t)
-        turn_mm(t, 1)
         inner_append(t, "io_", 0)
-        fill(1)
-        if not last:
-            ts(V("bo_"), V("psL", 0, 64), low + B0, A.add)
-        else:
-            ts(V("sa", 0, 64), V("psL", 0, 64), low + B0, A.add)
-            ts(V("sa", 64, 128), V("psL", 0, 64), low + 5120.0, A.add, 0.5, A.mult)
-            tt(V("sa", 128, 192), V("sa", 0, 64), V("sa", 64, 128), A.min)
-            cp(V("bo_"), V("sa", 128, 192))
-        for h in range(2):
-            act(half("old", h), G(V("ft", Z0, Z0 + B0 + t * F), offs("bo_", 0, h, 2)))
-        turn_out(t, 1)
-        fill(5)
-        mm(lists("psL", "zw", "old"))
-        old_sums()
+        walk(lambda i, n: tt(part("mk", i, n), G(V(RC[t]), offs("so", 0, i, n)), part("p1", i, n), A.min),
+             lambda i, n: tt(part("mk", i, n), G(it_window(t), offs("io_", 0, i, n)), part("p2", i, n), A.min),
+             pre,
+             lambda h: ts(offs("io_", 0, h, 2), V("psL%d" % h, 0, 32), low + I0, A.add),
+             conv2, V("ft", Z0, Z0 + B0 + t * F), ("bo_", 0))
         if last:
-            ts(V("yu"), V("rcb"), float(B0), A.add)
-            stage("i", "yu")
+            inner_out(0)
+            fill(2)
+            inner_out(1)
         far_lists(t, "fao", V("fo"))
         finish(t, "fo")
 
-    base = float(R0 + 3 * F)
-    ts(half("p1", 0), G(V("jj"), offs("so", 0, 0, 2)), base, A.add)
-    act(half("p1", 1), G(V("jj"), offs("so", 0, 1, 2)), bias=base)
-    stage("n", "p1", rows=(0, 128, 16))
-    dma([("y", V("yu"), D("l_i"))])
+    def plain(i):
+        tt(quad("rca", i), quad("p2", i), V(banks[i], 0, 256), A.min)
+        if i % 2:
+            dma([("y", X(T.yi[:, 256 * i - 256:256 * i + 256]), half("rca", i // 2))])
+
     for h in range(2):
-        cp(half("p2", h), half("yu", h))
-        act(V("psA%d" % h), half("p2", h), scale=0.5, bias=1792.0)
-    for h in range(2):
-        tt(half("rca", h), half("p2", h), V("psA%d" % h), A.min)
-        dma([("y", X(T.yi[:, 512 * h:512 * h + 512]), half("rca", h))])
+        dma([("ys"[h], half("yu", h), (T.l_i[:, 64 * h:64 * h + 64, :], [("l_i", 0, N + 2)]))])
+    for i in range(4):
+        cp(quad("p2", i), quad("yu", i))
+        act(V(banks[i], 0, 256), quad("p2", i), scale=0.5, bias=1792.0)
+        if i:
+            plain(i - 1)
+    plain(3)
     dma([("s", X(T.yb[:]), D("l_y"))])
-    dma([("y", X(T.yn[:]), D("l_n"))])
+    dma([("s", X(T.yn[:]), D("l_n"))])
     totals.update(count)
     for sem, val in totals.items():
         need("g", (sem, val, {}))

@@ -7,41 +7,49 @@ N, R0, I0, B0, F, CAP, RO = 8, 256, 1152, 1536, 1024, 144, 4
 CM = B0 + 3 * F
 Z0 = 16
 RN, KY, WE = R0, R0 + 64, R0 + 128
-IO, BO, W1 = I0, I0 + 64, I0 + 128
+IO, BO = 0, 64
 TW = 256
 LOW = 8192.0
 QB = 49152.0
 FB = 192.0
 OK = 65536.0
-PE_SLOTS = (5, 6, 7)
-TURN = (4, 5, 6, 7)
-DIAG = (-512.0, -1536.0, -2560.0, -3584.0, -4608.0, OK, OK / 2, 3.0)
+HALVES = (1, 2, 3)
+EARLY = (3, 5)
+GAP = (3, 3, 1, 2, 1, 1)
+NV_ROOT, NV_LAST = 4, 6
+BETWEEN = "10 11 v0 12 13 20 21 n1 22 23"
+SLOT = [(OK + q * CM) / (1 if q < 4 else 2) for q in range(N)]
+DIAG = [-512.0, -1536.0, -2560.0, -3584.0, -4608.0, 3.0] + SLOT
 
 SB = lambda n, d="float32", p=128: ("sbuf", [p, n], d)
-BF, I32, U16 = "bfloat16", "int32", "uint16"
+BF, F16, I32, U16 = "bfloat16", "float16", "int32", "uint16"
 SCRATCH = {
-    "ft": SB(Z0 + 8 * CM, BF), "tm": SB(16 * TW), "it": SB(I0 + 4096), "rt": SB(R0), "rh": SB(R0), "rca": SB(F), "rcb": SB(F),
-    "p1": SB(F), "p2": SB(F), "mk": SB(F, "float16"), "old": SB(F, BF), "far": SB(F, BF), "qn": SB(F, BF),
+    "ft": SB(Z0 + 8 * CM, BF), "tm": SB(16 * TW, BF), "it": SB(I0 + 4096), "rt": SB(R0), "rca": SB(F), "rcb": SB(F),
+    "p1": SB(F, F16), "p2": SB(F, F16), "mk": SB(F, F16), "mr": SB(F, F16), "gs": SB(F, F16),
+    "old": SB(F, BF), "far": SB(F, BF), "qn": SB(F, BF),
     "hr": SB(R0, I32), "hi": SB(I0, I32), "hn": SB(64, I32), "hb": SB(B0, BF), "hx": SB(F, I32, 8), "hxb": SB(F, BF, 8),
-    "e1": SB(WE, U16), "e2": SB(WE, U16), "m1": SB(W1, U16), "m2": SB(64, U16), "n1": SB(W1, U16), "n2": SB(64, U16),
-    "jj": SB(TW), "pi": SB(8, I32), "col": SB(16),
-    "zw": SB(144, BF), "zw3": SB(144, BF), "zs": SB(144, "float16"), "z8": SB(144, BF, 8),
-    "id1": SB(256, BF), "idf": SB(128), "dg": SB(128 * len(DIAG), BF), "bo": SB(128, BF), "lo": SB(128, BF),
+    "e1": SB(WE, U16), "e2": SB(WE, U16), "j1": SB(128, U16), "j2": SB(128, U16), "k1": SB(64, U16), "k2": SB(64, U16),
+    "oi": SB(I0, I32), "jj": SB(TW), "jb": SB(TW, BF), "pi": SB(8, I32), "col": SB(16),
+    "zw": SB(144, BF), "zw3": SB(144, BF), "zs": SB(144, F16), "z8": SB(144, BF, 8),
+    "id1": SB(128, BF), "idf": SB(128), "idp": SB(128, F16), "idn": SB(128, F16), "dg": SB(128 * len(DIAG), BF),
+    "bo": SB(128, BF), "lo": SB(128, BF),
     "rst": SB(512, BF), "fl": SB(64), "fn": SB(64), "fm": SB(128), "fah": SB(64), "fao": SB(64),
     "et": SB(16), "mc": SB(16), "bc": SB(16),
-    "cq": SB(128, BF), "oh": SB(512, BF), "sc": SB(512, BF), "cm": SB(512, BF),
+    "cq": SB(192, BF), "oh": SB(512, BF), "sc": SB(512, BF), "cm": SB(512, BF),
     "wki": SB(64, I32), "wkf": SB(64), "kb": SB(128, I32), "kf": SB(128), "ko": SB(128, U16), "kd": SB(128, U16),
     "wj": SB(64, I32), "sb": SB(128, I32), "sa": SB(192), "so": SB(64, U16), "io_": SB(64, U16), "bo_": SB(64, U16),
-    "hv": SB(128, I32), "hf": SB(64), "hq": SB(192, BF), "fo": SB(64, U16), "yu": SB(F, U16), "yb_": SB(F, BF), "yn_": SB(64),
+    "hv": SB(128, I32), "hf": SB(64), "hq": SB(128, BF), "fo": SB(64, U16), "yu": SB(F, F16), "yb_": SB(F, BF), "yn_": SB(64),
 }
 for _k in ("A0", "A1", "L0", "L1", "K", "Q", "X0", "X1"):
     SCRATCH["ps" + _k] = ("psum", [128, 512], "float32")
-MSG = {"b": (B0 // 8, BF), "e": (WE // 8, U16), "m": (W1 // 8, U16), "k": (8, U16),
-       "i": (F // 8, U16), "y": (F // 8, BF), "n": (F // 128, "float32")}
+MSG = {"b": (B0 // 8, BF), "e": (WE // 8, U16), "t": (I0 // 8, I32), "j": (128, U16), "k": (64, U16),
+       "i": (F // 8, F16), "n": (64, "float32"), "y": (F // 8, BF)}
+WHOLE = "jkn"
 for _k, (_n, _d) in MSG.items():
-    SCRATCH["s_" + _k] = ("dram", [N, 128, _n], _d)
+    if _k not in WHOLE:
+        SCRATCH["s_" + _k] = ("dram", [N, 128, _n], _d)
     SCRATCH["l_" + _k] = ("dram", [N, 128, _n], _d)
-SEMAPHORES = ["cv", "cs", "ct", "cg"] + ["d%d" % i for i in range(70)] + ["arr_" + k for k in MSG] + ["out_" + k for k in MSG]
+SEMAPHORES = ["cv", "cs", "ct", "cg"] + ["d%d" % i for i in range(80)] + ["arr_" + k for k in MSG] + ["out_" + k for k in MSG] + ["far_b"]
 
 
 def routes(T, topo):
@@ -80,6 +88,16 @@ def first_masks(a, T, topo, way):
     return out
 
 
+def fan(a, T, topo, way):
+    hub = [way[a, b] for b in T.cores if way[a, b] in topo.cores_of(a)][0]
+    far = [b for b in T.cores if b not in topo.cores_of(a)]
+    eoff = topo.engines(hub, far[0])
+    eon = [e for e in topo.engines(hub, a) if e not in eoff]
+    es = dict(zip(far, eoff[::2] + eoff[1::2]))
+    es.update(zip([b for b in T.cores if b not in far], eon))
+    return hub, es
+
+
 def relay_engines(c, b, topo):
     return topo.engines(c, b)[::2]
 
@@ -92,12 +110,21 @@ def relay_program(g, core, T, topo, way):
     n_in = len(first_masks(a, T, topo, way)[b])
     es = relay_engines(core, b, topo)
     rid, pid = topo.addr(b, core)
+    hub, fes = fan(a, T, topo, way)
     slot = T.rank_of(a)
-    for k in MSG:
-        g.wait_ge(T.sem["arr_" + k], n_in)
-        g.remote_dma(T["l_" + k][slot], T["l_" + k][slot], T.sem["arr_" + k], T.sem["out_" + k], pid, rid, bits(es))
-    for k in MSG:
-        g.wait_ge(T.sem["out_" + k], len(es))
+    mine = [k for k in MSG if k not in WHOLE or hub == core]
+    for k in mine:
+        piece = T["l_" + k][slot]
+        if k in WHOLE:
+            g.wait_ge(T.sem["arr_" + k], len(topo.engines(a, hub)))
+            g.remote_dma_fused([RemoteDMATransfer(dst_ids=[DstId(rid=topo.addr(c, core)[0], pnc=topo.addr(c, core)[1])],
+                                                  dma_engine_mask=bits([fes[c]]), remote_sem=T.sem["arr_" + k], src=piece, dst=piece)
+                                for c in T.cores], local_sem=T.sem["out_" + k])
+        else:
+            g.wait_ge(T.sem["arr_" + k], n_in)
+            g.remote_dma(piece, piece, T.sem["far_b" if k == "b" else "arr_" + k], T.sem["out_" + k], pid, rid, bits(es))
+    for k in mine:
+        g.wait_ge(T.sem["out_" + k], N if k in WHOLE else len(es))
 
 
 def rank_program(g, core, T, topo):
@@ -207,6 +234,8 @@ def rank_program(g, core, T, topo):
         note("t", rd, wr, ("ct", count["ct"], dict(known["t"])))
 
     def dma(items):
+        if not items:
+            return
         sem = "d%d" % nd[0]
         nd[0] += 1
         clock = {}
@@ -220,6 +249,7 @@ def rank_program(g, core, T, topo):
             note("dma", i[1], o[1], (sem, totals[sem], clock))
 
     masks = first_masks(core, T, topo, way)
+    own = (16 * rank, 16 * rank + 16)
 
     def send(k):
         order("g", [("s_" + k, 0, N)], [])
@@ -234,21 +264,35 @@ def rank_program(g, core, T, topo):
         g.remote_dma_fused(trs, local_sem=T.sem["out_" + k])
         totals["out_" + k] = sum(len(m) for m in masks.values())
 
-    n_arr = 0
-    for a in T.cores:
-        if a != core:
-            n_arr += len(first_masks(a, T, topo, way)[core]) if way[a, core] is None else len(relay_engines(way[a, core], core, topo))
-    for k in MSG:
-        totals["arr_" + k] = n_arr
-        for a in range(N):
-            if a != rank:
-                note("far", [], [("l_" + k, a, a + 1)], ("arr_" + k, n_arr, {}))
-    own = (16 * rank, 16 * rank + 16)
+    def W(name):
+        return (T[name], [(name, 0, T[name].shape[1])])
 
-    def stage(k, src):
-        dma([("y", D("s_" + k), V(src))])
-        dma([("y", D("l_" + k, rank, rank + 1), V(src, p=own))])
-        send(k)
+    def staged(k, t):
+        dma([("y", D("s_" + k), (t[0][:], t[1]))])
+        dma([("y", D("l_" + k, rank, rank + 1), (t[0][own[0]:own[1], :], t[1]))])
+
+    def hand(k, src):
+        hub = fan(core, T, topo, way)[0]
+        es = topo.engines(core, hub)
+        rid, pid = topo.addr(hub, core)
+        order("g", src[1], [])
+        g.remote_dma(T["l_" + k][rank], src[0], T.sem["arr_" + k], T.sem["out_" + k], pid, rid, bits(es))
+        totals["out_" + k] = len(es)
+        note("dma", src[1], [], ("out_" + k, len(es), dict(known["g"])))
+
+    def rows_of(k):
+        return (T["l_" + k][:, own[0]:own[1], :], [("l_" + k, 0, N)])
+
+    near = [a for a in range(N) if way[T.cores[a], core] is None]
+    late = [a for a in range(N) if a not in near]
+    n_near = sum(len(first_masks(T.cores[a], T, topo, way)[core]) for a in near if a != rank)
+    totals["far_b"] = sum(len(relay_engines(way[T.cores[a], core], core, topo)) for a in late)
+    for k in MSG:
+        totals["arr_" + k] = N if k in WHOLE else n_near if k == "b" else n_near + totals["far_b"]
+        for a in range(N):
+            if a != rank or k in WHOLE:
+                sem = "far_b" if k == "b" and a in late else "arr_" + k
+                note("far", [], [("l_" + k, a, a + 1)], (sem, totals[sem], {}))
 
     dma([("s", V("hx"), X(T.x0[:]))])
     dma([("y", V("hr"), X(T.rtab[:])), ("s", V("hn"), X(T.rn0[:]))])
@@ -265,11 +309,11 @@ def rank_program(g, core, T, topo):
     ms(V("lo"), -1.0)
     ms(V("ft", 0, Z0), 0.0)
     diag, grp = [[-1, 128]], [[16, 8], [0, 16]]
-    ID = V("id1", 0, 128)
-    sel(V("id1"), V("rst", 0, 256), [[0, 2], [-1, 128]], A.is_equal, 0.0, 0, 1)
+    ID = V("id1")
+    sel(ID, V("rst", 0, 128), diag, A.is_equal, 0.0, 0, 1)
     sel(V("bo"), V("rst", 0, 128), [[-16, 8], [0, 16]], A.is_ge, 0.0, 0, 1)
-    send("b")
     sel(V("bo"), V("bo"), grp, A.is_ge, 0.0, 15, -1)
+    send("b")
     sel(V("lo"), V("lo"), grp, A.is_ge, 0.0, 15, -1)
     sel(V("lo"), V("lo"), diag, A.is_gt, 0.0, 0, 1)
     sel(V("lo"), V("lo"), diag, A.not_equal, -1024.0, 0, 1)
@@ -294,7 +338,10 @@ def rank_program(g, core, T, topo):
         return V("dg", 128 * i, 128 * i + 128)
 
     def tblock(d):
-        act(V("tm", d * TW, (d + 1) * TW), V("jj"), scale=V("mc", d, d + 1), bias=V("bc", d, d + 1))
+        if d < 12:
+            act(V("tm", d * TW, (d + 1) * TW), V("jj"), scale=V("mc", d, d + 1), bias=V("bc", d, d + 1))
+        else:
+            ts(V("tm", d * TW, (d + 1) * TW), V("jb"), V("mc", d, d + 1), A.mult, V("bc", d, d + 1), A.add)
 
     def lists(out, z, src, start=True, stop=True, h=None, at=None):
         lo, w = (0, 64) if h is None else (32 * h, 32)
@@ -302,11 +349,15 @@ def rank_program(g, core, T, topo):
         return [(V(out, at, at + w), V(z, 15 - r, 143 - r), V(src, 16 * lo + r, 16 * (lo + w), 16), start and r == 0, stop and r == 15)
                 for r in range(16)]
 
-    def rows(out, z, src, start=True, stop=True):
-        return [(V(out, 0, 64), V(z, 15 - r, 143 - r), V(src, 64 * r, 64 * r + 64), start and r == 0, stop and r == 15) for r in range(16)]
+    def rows(out, z, src):
+        return [(V(out, 0, 64), V(z, 15 - r, 143 - r), V(src, 64 * r, 64 * r + 64), r == 0, r == 15) for r in range(16)]
 
-    def half(name, h, base=0):
-        return V(name, base + 512 * h, base + 512 * h + 512)
+    def part(name, i, n):
+        w = F // n
+        return V(name, w * i, w * i + w)
+
+    def half(name, h):
+        return part(name, h, 2)
 
     def quad(name, h):
         return V(name, 256 * h, 256 * h + 256)
@@ -322,17 +373,26 @@ def rank_program(g, core, T, topo):
         cp(V("ko"), V("kf"))
 
     todo = []
-    turns = []
+    side = []
 
     def fill(n):
-        for _ in range(n):
-            if todo:
-                todo.pop(0)()
+        while todo and (n > 0 or todo[0][2] == 0):
+            job, lo, hi, uncut = todo[0]
+            w = hi - lo if uncut else min(n, hi - lo)
+            job(lo, lo + w)
+            n -= w
+            if lo + w == hi:
+                todo.pop(0)
+            else:
+                todo[0] = (job, lo + w, hi, uncut)
 
-    def turn(n):
+    def later(job, w):
+        todo.append((lambda lo, hi: job(), 0, w, True))
+
+    def aside(n=1):
         for _ in range(n):
-            if turns:
-                turns.pop(0)()
+            if side:
+                side.pop(0)()
 
     def far_lists(t, fa, out):
         C = B0 + t * F
@@ -343,133 +403,139 @@ def rank_program(g, core, T, topo):
         act(V("hf"), H, scale=1.0 / 1024.0)
         for i in range(2):
             act(V("hq", 64 * i, 64 * i + 64), H, scale=1.0 / (1024.0 * P), bias=FB - 0.5 + 0.5 / P + i * (P - C) / P)
-        turn(1)
+        aside()
         for q in range(N):
             ts(V("oh", 64 * q, 64 * q + 64), V("hv", 64, 128), float(q), A.is_equal)
         mm([(V("psX%d" % h, 0, 256), V("lo"), quad("oh", h), True, False) for h in range(2)])
         run("v", V("sc"), [V("rst"), V("oh")], lambda: g.vector.tensor_tensor_scan(T.sc[:], T.rst[:], T.oh[:], 0.0, A.mult, A.add))
         for h in range(2):
             mm([(V("psX%d" % h, 0, 256), V("bo"), quad("sc", h), False, True)])
-        ts(V("hq", 128, 192), V("hv", 64, 128), -1.0, A.mult)
-        mm([(S, V("idf"), V("hf"), True, False), (S, DG(C - P), V("hq", 0, 64), False, False), (S, DG(-C), V("hq", 64, 128), False, False),
-            (S, DG(-CM), V("hq", 128, 192), False, False)])
-        fill(1)
+        mm([(S, V("idf"), V("hf"), True, False), (S, DG(C - P), V("hq", 0, 64), False, False), (S, DG(-C), V("hq", 64, 128), False, False)])
+        fill(GAP[2])
         ts(quad("cm", 0), V("psX0", 0, 256), float(CAP - 1023), A.is_lt, 0.5, A.add)
         act(quad("cm", 1), V("psX1", 0, 256), scale=-1.0, bias=CAP - 1023.5, func=AF.Sign)
-        turn(1)
-        mm([(S, DG(OK / 2 if q >= 4 else OK), V("cm", 64 * q, 64 * q + 64), False, q == N - 1) for q in range(N)])
-        turn(8)
-        fill(1)
-        ts(out, S, Z0 - OK + FB * P, A.add)
+        mm([(S, DG(SLOT[q]), V("cm", 64 * q, 64 * q + 64), False, q == N - 1) for q in range(N)])
+        fill(GAP[3])
+        ts(out, S, Z0 - OK + FB * P - sum(SLOT[:4]) / 2 + sum(SLOT[4:]), A.add)
+
+    def nothing(h):
+        pass
 
     def walk(pick1, pick2, pre, conv1, conv2, old_win, bo):
         for h in range(2):
             pre(h)
             pick1(h, 2)
-            mm(lists("psL%d" % h, "zs", "mk", start=pre is nothing, h=h, at=0))
+            mm(lists("psL%d" % h, "zs", "mr", start=pre is nothing, h=h, at=0))
         conv1(0)
         pre(0)
         pick2(0, 2)
-        turn(1)
         mm(lists("psL0", "zs", "mk", start=pre is nothing, h=0, at=0))
         conv1(1)
         pre(1)
         pick2(2, 4)
         conv2(0)
+        aside()
         act(half("old", 0), G(old_win, offs(bo[0], bo[1], 0, 2)))
         pick2(3, 4)
         mm(lists("psL1", "zs", "mk", start=pre is nothing, h=1, at=0))
         mm(lists("psL0", "zw", "old", h=0))
-        fill(1)
+        fill(GAP[0])
         conv2(1)
         cp(quad("old", 2), G(old_win, offs(bo[0], bo[1], 2, 4)))
         act(quad("old", 3), G(old_win, offs(bo[0], bo[1], 3, 4)))
-        turn(1)
+        aside()
         mm(lists("psL0", "zw", "old", h=1))
-        fill(1)
+        aside()
+        fill(GAP[1])
 
-    def nothing(h):
-        pass
+    def fill_b(ranks, ks):
+        items = []
+        for k in ks:
+            for a in ranks:
+                if a - 1 in ranks and a != k:
+                    continue
+                n = 1
+                while a + n in ranks and a + n != k:
+                    n += 1
+                p0 = 16 * ((a - k) % N)
+                dst = V("ft", Z0 + k * CM, Z0 + k * CM + B0, p=(p0, p0 + 16 * n))[0]
+                items.append(("y", (dst, [("ft", Z0 + k * CM + a, Z0 + k * CM + a + n)]), D("l_b", a, a + n)))
+        dma(items)
 
-    def part(name, i, n):
-        w = F // n
-        return V(name, w * i, w * i + w)
+    def fill_new(lo, w, ks):
+        items = []
+        for k in ks:
+            c0 = Z0 + k * CM + lo
+            items.append(("y", V("ft", c0, c0 + w, p=(0, 128 - 16 * k)), V("ft", Z0 + lo, Z0 + lo + w, p=(16 * k, 128))))
+            items.append(("y", V("ft", c0, c0 + w, p=(128 - 16 * k, 128)), V("ft", Z0 + lo, Z0 + lo + w, p=(0, 16 * k))))
+        dma(items)
 
     cp(half("hxb", 0), half("hx", 0))
     cp(V("e1", RN, RN + 64), V("hn"))
-    cp(V("rh"), V("hr"))
     cp(half("hxb", 1), half("hx", 1))
     mm(lists("psK", "z8", "hxb"))
     cp(V("e1", 0, R0), V("hr"))
     for d in range(0, 4):
         tblock(d)
     for h in range(2):
-        act(half("p1", h), G(V("rh"), offs("e1", RN, h, 2)))
+        act(half("p1", h), G(V("hr"), offs("e1", RN, h, 2)))
     cp(V("wki"), V("psK", 0, 64))
-    ts(V("e1", KY, KY + 64), V("psK", 0, 64), 1.0 / 1024.0, A.mult)
-    stage("e", "e1")
-    iota(V("fm"), [[0, 8], [16, 16]])
-    for h in range(2):
-        iota(V("cq", 64 * h, 64 * h + 64), [[-15 * TW * (h + 1), 4], [0, 16]])
     ts(V("sb", 0, 64), V("wki"), 10, A.logical_shift_right, 15, A.bitwise_and)
     ts(V("sb", 64, 128), V("wki"), 14, A.logical_shift_right, 15, A.bitwise_and)
     cp(V("kd"), V("sb"))
+    ts(V("e1", KY, KY + 64), V("psK", 0, 64), 1.0 / 1024.0, A.mult)
+    staged("e", W("e1"))
+    send("e")
+    staged("t", X(T.itab))
+    send("t")
+    iota(V("fm"), [[0, 8], [16, 16]])
+    for h in range(3):
+        iota(V("cq", 64 * h, 64 * h + 64), [[-15 * TW * 2 ** h, 4], [0, 16]])
     for h in range(2):
         act(half("p2", h), G(V("et"), offs("kd", 64, h, 2)))
-    for d in range(4, 7):
+    for d in range(4, 8):
         tblock(d)
-
-    def home_consts():
-        cp(V("idf"), ID)
-        for c in (-512, -1536, -CM, OK, OK / 2):
-            ts(DG(c), ID, float(c), A.mult)
-
-    for h in range(2):
-        todo.append(lambda h=h: cp(V("m1", h * I0 // 2, (h + 1) * I0 // 2), V("hi", h * I0 // 2, (h + 1) * I0 // 2)))
-    todo.append(home_consts)
-    walk(lambda i, n: tt(part("mk", i, n), G(V("et"), offs("kd", 0, i, n)), part("p1", i, n), A.min),
-         lambda i, n: tt(part("mk", i, n), G(V("hi"), offs("m1", IO, i, n)), part("p2", i, n), A.min),
+    later(lambda: [ts(DG(c), ID, float(c), A.mult) for c in [-512, -1536] + SLOT[:4]], GAP[0])
+    later(lambda: [cp(V("idf"), ID)] + [ts(DG(c), ID, float(c), A.mult) for c in SLOT[4:]], GAP[1])
+    walk(lambda i, n: tt(part("mr", i, n), G(V("et"), offs("kd", 0, i, n)), part("p1", i, n), A.min),
+         lambda i, n: tt(part("mk", i, n), G(V("hi"), offs("j1", IO, i, n)), part("p2", i, n), A.min),
          nothing,
-         lambda h: cp(offs("m1", IO, h, 2), V("psL%d" % h, 0, 32)),
-         lambda h: cp(offs("m1", BO, h, 2), V("psL%d" % h, 0, 32)),
-         V("hb"), ("m1", BO))
-    stage("m", "m1")
-    fill(1)
+         lambda h: cp(offs("j1", IO, h, 2), V("psL%d" % h, 0, 32)),
+         lambda h: cp(offs("j1", BO, h, 2), V("psL%d" % h, 0, 32)),
+         V("hb"), ("j1", BO))
+    hand("j", V("j1"))
+    fill_b(near, range(EARLY[0]))
     ms(V("rst", 0, 512, 64), 0.0)
-    far_lists(0, "fah", V("m2"))
-    stage("k", "m2")
-    for d in range(7, 16):
+    far_lists(0, "fah", V("k1"))
+    hand("k", V("k1"))
+    cp(V("jb"), V("jj"))
+    for d in range(8, 16):
         tblock(d)
 
-    def fill_far(lo, w, src, ks):
-        items = []
-        for k in ks:
-            c0 = Z0 + k * CM + lo
-            items.append(("y", V("ft", c0, c0 + w, p=(0, 128 - 16 * k)), src(k, N)))
-            if k:
-                items.append(("y", V("ft", c0, c0 + w, p=(128 - 16 * k, 128)), src(0, k)))
-        if items:
-            dma(items)
-
-    rest = [k for k in range(1, N) if k not in PE_SLOTS]
-    landed = lambda a, b: D("l_b", a, b)
-    fill_far(0, B0, landed, [0])
     dma([("y", V("e2"), D("l_e"))])
-    fill_far(0, B0, landed, rest[:2])
-    dma([("y", V("n1"), D("l_m"))])
-    fill_far(0, B0, landed, rest[2:])
-    dma([("y", V("n2"), D("l_k"))])
+    fill_b(late, [0])
+    fill_b(near, range(EARLY[0], EARLY[1]))
+    dma([("y", V("oi"), D("l_t"))])
+    need("y", ("out_k", totals["out_k"], {}))
+    dma([("y", V("j2"), rows_of("j"))])
+    fill_b(late, range(1, EARLY[1]))
+    fill_b(range(N), range(EARLY[1], N))
+    dma([("y", V("k2"), rows_of("k"))])
+    ts(V("fm"), V("fm"), C_(R_), A.add)
+    ts(V("wki"), V("e2", KY, KY + 64), 1024.0, A.mult)
+    key_lists()
     ts(C_(WT3), C_(R_), 6144.0, A.mult, 3072.0, A.add)
     ts(C_(GA), C_(G16), -64.0, A.mult, 8192.0, A.add)
     ts(C_(R64), C_(R_), 64.0, A.mult)
     ts(V("zw3"), V("jj", 0, 144), C_(ZC), A.is_equal, C_(WT3), A.mult)
-    for c in (3, -2560, -3584):
+    for c in (3, -2560, -3584, -4608):
         ts(DG(c), ID, float(c), A.mult)
+    cp(V("idp"), ID)
+    ts(V("idn"), ID, -1.0, A.mult)
     ts(V("fao"), V("fl"), 1024.0, A.mult, C_(GA), A.add)
     ts(V("fn"), V("jj", 0, 64), C_(R64), A.add)
-    ts(V("fm"), V("fm"), C_(R_), A.add)
 
-    SCALE = (1.0, 1.0, 2.0, 2.0)
+    SCALE = (1.0, 1.0, 2.0, 4.0)
     BIAS = (0.0, 1024.0, 2048.0, 4096.0)
     RC = ("rt", "rca", "rcb", "rca")
 
@@ -480,23 +546,28 @@ def rank_program(g, core, T, topo):
     def it_window(t):
         return V("it", 0, I0 + 4096 if t == 3 else I0 + t * F)
 
-    def root_append(t, off, base):
-        for i in range(4):
-            todo.append(lambda i=i: tt(quad(RC[t + 1], i), G(V(RC[t]), offs(off, base, i, 4)), quad("p1", i), A.max))
+    def root_append(t, off, base, n=8):
+        todo.append((lambda a, b: tt(V(RC[t + 1], 128 * a, 128 * b), G(V(RC[t]), V(off, base + 8 * a, base + 8 * b)),
+                                     V("p1", 128 * a, 128 * b), A.max), 0, n, False))
 
-    def inner_append(t, off, base):
-        for i in range(4):
+    def inner_append(t, off, base, n=8):
+        def job(a, b):
             if t < 2:
-                o = V("it", I0 + t * F + 256 * i, I0 + t * F + 256 * i + 256)
+                o = V("it", I0 + t * F + 128 * a, I0 + t * F + 128 * b)
             elif t == 2:
-                o = V("it", I0 + 2048 + 512 * i, I0 + 2048 + 512 * i + 512, 2)
+                o = V("it", I0 + 2048 + 256 * a, I0 + 2048 + 256 * b, 2)
             else:
-                o = quad("rcb", i)
-            todo.append(lambda i=i, o=o: tt(o, G(it_window(t), offs(off, base, i, 4)), quad("p2", i), A.max))
+                o = V("yu", 128 * a, 128 * b)
+            tt(o, G(it_window(t), V(off, base + 8 * a, base + 8 * b)), V("p2", 128 * a, 128 * b), A.max)
+        todo.append((job, 0, n, False))
 
-    def turned(k, c0, bank, copy):
-        mm([(V(bank), V("id1", 16 * k, 16 * k + 128), V("ft", Z0 + c0, Z0 + c0 + 512), True, True)])
-        copy(V("ft", Z0 + k * CM + c0, Z0 + k * CM + c0 + 512), V(bank))
+    def side_append(win, off, p, m, out, a):
+        lo = 128 * a
+        ps = V("psQ", 0, F - lo)
+        return [lambda: mm([(ps, V("idn"), V(m, lo), True, False), (ps, V("idp"), V(p, lo), False, False)]),
+                lambda: act(V("gs", lo), G(win, V(off, 8 * a))),
+                lambda: mm([(ps, V("idp"), V("gs", lo), False, True)]),
+                lambda: act(V(out, lo), ps)]
 
     def finish(t, off):
         last = t == RO - 1
@@ -511,7 +582,7 @@ def rank_program(g, core, T, topo):
         for h in range(2):
             mm([far3("A", h, True)])
         mm([far3("X", h, False) for h in range(2)] if last else lists("psK", "zw3", "far", start=False))
-        fill(1)
+        fill(GAP[4])
         qb = -(QB - 127.5 + t)
         ts(half("qn", 0), V("psA0"), -1.0, A.mult, qb, A.add)
         act(half("qn", 1), V("psA1"), scale=-1.0, bias=qb)
@@ -520,13 +591,14 @@ def rank_program(g, core, T, topo):
                 mm([carry(h)])
             ts(half("yb_", 0), V("psX0"), QB + t, A.add)
             act(half("yb_", 1), V("psX1"), bias=QB + t)
-            stage("y", "yb_")
+            staged("y", W("yb_"))
             mm(rows("psQ", "zw", "yb_"))
             cp(V("wj"), V("psQ", 0, 64))
         else:
             mm(lists("psQ", "zw", "qn"))
             for h in range(2):
                 mm([base("X", h), far3("X", h, False), carry(h)])
+            fill(GAP[5])
             cp(V("wki"), V("psK", 0, 64))
             act(V("wkf"), V("psK", 0, 64), bias=1024.0 * 256.0 * (QB + t))
             key_lists()
@@ -538,61 +610,44 @@ def rank_program(g, core, T, topo):
         tt(V("sa", 128, 192), V("sa", 0, 64), V("sa", 64, 128), A.max)
         if last:
             ts(V("yn_"), V("sa", 128, 192), float(R0 + t * F), A.add)
-            stage("n", "yn_")
+            hand("n", V("yn_"))
+            send("y")
             return
-        fill(8)
+        fill(16)
         cp(V("so"), V("sa", 128, 192))
+        for who, i in BETWEEN.split():
+            i = int(i)
+            if who in "12":
+                mask_q("p" + who, t + 1, i)
+                continue
+            c0 = C + 512 * i
+            if who == "n":
+                act(V("ft", Z0 + c0, Z0 + c0 + 512), V("psX%d" % i), bias=QB + t)
+            else:
+                ts(V("ft", Z0 + c0, Z0 + c0 + 512), V("psX%d" % i), QB + t, A.add)
+            if i:
+                fill_new(C, F, [k for k in range(1, N) if k not in HALVES])
+            fill_new(c0, 512, HALVES)
 
-        def new_half(h):
-            c0 = C + 512 * h
-            act(V("ft", Z0 + c0, Z0 + c0 + 512), V("psX%d" % h), bias=QB + t)
-            fill_far(c0, 512, lambda a, b: V("ft", Z0 + c0, Z0 + c0 + 512, p=(16 * a, 16 * b)),
-                     [k for k in range(1, N) if h == 0 or k not in TURN])
-
-        for i in range(2):
-            mask_q("p1", t + 1, i)
-        new_half(0)
-        for i in range(2, 4):
-            mask_q("p1", t + 1, i)
-        for i in range(4):
-            mask_q("p2", t + 1, i)
-        new_half(1)
-        for i, k in enumerate(TURN):
-            turns.append(lambda i=i, k=k: turned(k, C + 512, ("psQ", "psK")[i % 2], act))
-
-    ts(V("wki"), V("e2", KY, KY + 64), 1024.0, A.mult)
-    key_lists()
     for name in ("p1", "p2"):
         for i in range(4):
             mask_q(name, 0, i)
-    banks = ("psA0", "psX0", "psA1", "psX1")
-    n, NA, NV = 0, 3, 6
-    for k in PE_SLOTS:
-        for j in range(B0 // 512):
-            turned(k, 512 * j, banks[n % 4], act if n >= NV else cp)
-            n += 1
-            if n == NA:
-                ts(V("rt"), V("e2", 0, R0), float(-I0), A.add)
-                root_append(0, "e2", RN)
-                fill(4)
-    act(half("old", 0), G(V("ft", Z0, Z0 + B0), offs("n1", BO, 0, 2)))
-    act(half("old", 1), G(V("ft", Z0, Z0 + B0), offs("n1", BO, 1, 2)))
-    ts(V("it", 0, I0), V("n1", 0, I0), float(-B0), A.add)
-    inner_append(0, "n1", IO)
-    fill(1)
-    finish(0, "n2")
-
-    def inner_out(h):
-        ts(half("yu", h), half("rcb", h), float(B0), A.add)
-        dma([("y", (T.s_i[:, 64 * h:64 * h + 64, :], [("s_i", 4 * h, 4 * h + 4)]), half("yu", h)),
-             ("y", (T.l_i[rank, 64 * h:64 * h + 64, :], [("l_i", N + h, N + h + 1)]), V("yu", 512 * h, 512 * h + 512, p=own))])
-        if h:
-            send("i")
+    ts(V("rt"), V("e2", 0, R0), float(-I0), A.add)
+    root_append(0, "e2", RN)
+    fill(4)
+    fill(4)
+    ts(V("it", 0, I0), V("oi"), float(-B0), A.add)
+    for h in range(2):
+        act(half("old", h), G(V("ft", Z0, Z0 + B0), offs("j2", BO, h, 2)))
+    inner_append(0, "j2", IO)
+    fill(4)
+    fill(4)
+    finish(0, "k2")
 
     for t in range(1, RO):
         low = 15.0 * (LOW * SCALE[t] - BIAS[t])
         last = t == RO - 1
-        s0 = 64 if SCALE[t] > 1 else 0
+        s0 = 64 * (t - 1)
 
         def pre(h):
             mm([(V("psL%d" % h, 0, 32), ID, V("cq", s0 + 32 * h, s0 + 32 * h + 32), True, False)])
@@ -608,35 +663,33 @@ def rank_program(g, core, T, topo):
                 cp(offs("bo_", 0, h, 2), V("sa", 128, 160))
 
         if not last:
-            root_append(t, "so", 0)
-        inner_append(t, "io_", 0)
-        walk(lambda i, n: tt(part("mk", i, n), G(V(RC[t]), offs("so", 0, i, n)), part("p1", i, n), A.min),
+            root_append(t, "so", 0, NV_ROOT)
+            inner_append(t, "io_", 0)
+            side.extend(side_append(V(RC[t]), "so", "p1", "mr", RC[t + 1], NV_ROOT))
+        else:
+            inner_append(t, "io_", 0, NV_LAST)
+            later(lambda: (staged("i", W("yu")), send("i")), 0)
+            st = side_append(it_window(t), "io_", "p2", "mk", "yu", NV_LAST)
+            side.extend([lambda: None, lambda: (st[0](), st[1]()), lambda: (st[2](), st[3]())])
+        walk(lambda i, n: tt(part("mr", i, n), G(V(RC[t]), offs("so", 0, i, n)), part("p1", i, n), A.min),
              lambda i, n: tt(part("mk", i, n), G(it_window(t), offs("io_", 0, i, n)), part("p2", i, n), A.min),
              pre,
              lambda h: ts(offs("io_", 0, h, 2), V("psL%d" % h, 0, 32), low + I0, A.add),
              conv2, V("ft", Z0, Z0 + B0 + t * F), ("bo_", 0))
-        if last:
-            inner_out(0)
-            fill(2)
-            inner_out(1)
         far_lists(t, "fao", V("fo"))
         finish(t, "fo")
 
-    def plain(i):
-        tt(quad("rca", i), quad("p2", i), V(banks[i], 0, 256), A.min)
+    dma([("y", V("yu"), D("l_i"))])
+    dma([("y", X(T.yn[:]), rows_of("n"))])
+    dma([("y", X(T.yb[:]), D("l_y"))])
+    for i, bank in enumerate(("psA0", "psX0", "psA1", "psX1")):
+        ps = V(bank, 0, 256)
+        ts(quad("p1", i), quad("yu", i), 0.5, A.mult, 1024.0, A.max)
+        ts(quad("p2", i), quad("yu", i), 0.25, A.mult, 1024.0, A.max)
+        mm([(ps, V("idp"), quad("yu", i), True, False), (ps, V("idn"), quad("p1", i), False, False), (ps, V("idn"), quad("p2", i), False, True)])
+        act(quad("rca", i), ps, bias=B0 + 2048.0)
         if i % 2:
-            dma([("y", X(T.yi[:, 256 * i - 256:256 * i + 256]), half("rca", i // 2))])
-
-    for h in range(2):
-        dma([("ys"[h], half("yu", h), (T.l_i[:, 64 * h:64 * h + 64, :], [("l_i", 0, N + 2)]))])
-    for i in range(4):
-        cp(quad("p2", i), quad("yu", i))
-        act(V(banks[i], 0, 256), quad("p2", i), scale=0.5, bias=1792.0)
-        if i:
-            plain(i - 1)
-    plain(3)
-    dma([("s", X(T.yb[:]), D("l_y"))])
-    dma([("s", X(T.yn[:]), D("l_n"))])
+            dma([("s", X(T.yi[:, 256 * i - 256:256 * i + 256]), half("rca", i // 2))])
     totals.update(count)
     for sem, val in totals.items():
         need("g", (sem, val, {}))

from concourse.bass import DstId, RemoteDMATransfer
from concourse.mybir import AluOpType, ActivationFunctionType

A = AluOpType
AF = ActivationFunctionType
N, R0, I0, B0, F, CAP, RO = 8, 256, 1152, 1536, 1024, 144, 4
CM = B0 + 3 * F
Z0 = 16
RN, KY, WE = R0, R0 + 64, R0 + 128
IO, BO = 0, 64
TW = 256
LOW = 8192.0
QB = 49152.0
FB = 192.0
OK = 65536.0
HALVES = (1, 2, 3)
EARLY = (3, 5)
GAP = (3, 3, 1, 2, 1, 1)
NV_ROOT, NV_LAST = 4, 6
BETWEEN = "10 11 v0 12 13 20 21 n1 22 23"
SLOT = [(OK + q * CM) / (1 if q < 4 else 2) for q in range(N)]
DIAG = [-512.0, -1536.0, -2560.0, -3584.0, -4608.0, 3.0] + SLOT

SB = lambda n, d="float32", p=128: ("sbuf", [p, n], d)
BF, F16, I32, U16 = "bfloat16", "float16", "int32", "uint16"
SCRATCH = {
    "ft": SB(Z0 + 8 * CM, BF), "tm": SB(16 * TW, BF), "it": SB(I0 + 4096), "rt": SB(R0), "rca": SB(F), "rcb": SB(F),
    "p1": SB(F, F16), "p2": SB(F, F16), "mk": SB(F, F16), "mr": SB(F, F16), "gs": SB(F, F16),
    "old": SB(F, BF), "far": SB(F, BF), "qn": SB(F, BF),
    "hr": SB(R0, I32), "hi": SB(I0, I32), "hn": SB(64, I32), "hb": SB(B0, BF), "hx": SB(F, I32, 8), "hxb": SB(F, BF, 8),
    "e1": SB(WE, U16), "e2": SB(WE, U16), "j1": SB(128, U16), "j2": SB(128, U16), "k1": SB(64, U16), "k2": SB(64, U16),
    "oi": SB(I0, I32), "jj": SB(TW), "jb": SB(TW, BF), "pi": SB(8, I32), "col": SB(16),
    "zw": SB(144, BF), "zw3": SB(144, BF), "zs": SB(144, F16), "z8": SB(144, BF, 8),
    "id1": SB(128, BF), "idf": SB(128), "idp": SB(128, F16), "idn": SB(128, F16), "dg": SB(128 * len(DIAG), BF),
    "bo": SB(128, BF), "lo": SB(128, BF),
    "rst": SB(512, BF), "fl": SB(64), "fn": SB(64), "fm": SB(128), "fah": SB(64), "fao": SB(64),
    "et": SB(16), "mc": SB(16), "bc": SB(16),
    "cq": SB(192, BF), "oh": SB(512, BF), "sc": SB(512, BF), "cm": SB(512, BF),
    "wki": SB(64, I32), "wkf": SB(64), "kb": SB(128, I32), "kf": SB(128), "ko": SB(128, U16), "kd": SB(128, U16),
    "wj": SB(64, I32), "sb": SB(128, I32), "sa": SB(192), "so": SB(64, U16), "io_": SB(64, U16), "bo_": SB(64, U16),
    "hv": SB(128, I32), "hf": SB(64), "hq": SB(128, BF), "fo": SB(64, U16), "yu": SB(F, F16), "yb_": SB(F, BF), "yn_": SB(64),
}
for _k in ("A0", "A1", "L0", "L1", "K", "Q", "X0", "X1"):
    SCRATCH["ps" + _k] = ("psum", [128, 512], "float32")
MSG = {"b": (B0 // 8, BF), "e": (WE // 8, U16), "t": (I0 // 8, I32), "j": (128, U16), "k": (64, U16),
       "i": (F // 8, F16), "n": (64, "float32"), "y": (F // 8, BF)}
WHOLE = "jkn"
for _k, (_n, _d) in MSG.items():
    if _k not in WHOLE:
        SCRATCH["s_" + _k] = ("dram", [N, 128, _n], _d)
    SCRATCH["l_" + _k] = ("dram", [N, 128, _n], _d)
SEMAPHORES = ["cv", "cs", "ct", "cg"] + ["d%d" % i for i in range(80)] + ["arr_" + k for k in MSG] + ["out_" + k for k in MSG] + ["far_b"]


def routes(T, topo):
    used = set(T.cores)
    way = {}
    world = range(128 * (1 + max(topo.host(c) for c in T.cores)))
    for a in T.cores:
        for b in T.cores:
            if a == b or topo.may_write(a, b):
                way[a, b] = None
                continue
            pool = topo.cores_of(a) if topo.host(a) == topo.host(b) else [c for c in world if topo.mates(c, b)]
            pool = [c for c in pool if c not in used and topo.die(c) == topo.die(a) and topo.may_write(a, c) and topo.may_write(c, b)]
            way[a, b] = pool[0]
            used.add(pool[0])
    return way


def bits(es):
    return sum(1 << e for e in es)


def first_masks(a, T, topo, way):
    hops = [(b, way[a, b] if way[a, b] is not None else b) for b in T.cores if b != a]
    off = [h for h in hops if h[1] not in topo.cores_of(a)]
    on = [h for h in hops if h[1] in topo.cores_of(a)]
    eoff = topo.engines(a, off[0][1])
    eon = [e for e in topo.engines(a, on[0][1]) if e not in eoff]
    out = {}
    for hs, es in ((off, eoff), (on, eon)):
        n = 1
        while 2 * n * len(hs) <= len(es):
            n *= 2
        for i, h in enumerate(hs):
            out[h[0]] = es[i * n:(i + 1) * n]
    return out


def fan(a, T, topo, way):
    hub = [way[a, b] for b in T.cores if way[a, b] in topo.cores_of(a)][0]
    far = [b for b in T.cores if b not in topo.cores_of(a)]
    eoff = topo.engines(hub, far[0])
    eon = [e for e in topo.engines(hub, a) if e not in eoff]
    es = dict(zip(far, eoff[::2] + eoff[1::2]))
    es.update(zip([b for b in T.cores if b not in far], eon))
    return hub, es


def relay_engines(c, b, topo):
    return topo.engines(c, b)[::2]


def relay_program(g, core, T, topo, way):
    pair = [k for k, v in way.items() if v == core]
    if not pair:
        return
    a, b = pair[0]
    n_in = len(first_masks(a, T, topo, way)[b])
    es = relay_engines(core, b, topo)
    rid, pid = topo.addr(b, core)
    hub, fes = fan(a, T, topo, way)
    slot = T.rank_of(a)
    mine = [k for k in MSG if k not in WHOLE or hub == core]
    for k in mine:
        piece = T["l_" + k][slot]
        if k in WHOLE:
            g.wait_ge(T.sem["arr_" + k], len(topo.engines(a, hub)))
            g.remote_dma_fused([RemoteDMATransfer(dst_ids=[DstId(rid=topo.addr(c, core)[0], pnc=topo.addr(c, core)[1])],
                                                  dma_engine_mask=bits([fes[c]]), remote_sem=T.sem["arr_" + k], src=piece, dst=piece)
                                for c in T.cores], local_sem=T.sem["out_" + k])
        else:
            g.wait_ge(T.sem["arr_" + k], n_in)
            g.remote_dma(piece, piece, T.sem["far_b" if k == "b" else "arr_" + k], T.sem["out_" + k], pid, rid, bits(es))
    for k in mine:
        g.wait_ge(T.sem["out_" + k], N if k in WHOLE else len(es))


def rank_program(g, core, T, topo):
    way = routes(T, topo)
    rank = T.rank_of(core)
    if rank is None:
        relay_program(g, core, T, topo, way)
        return

    Q = {"v": g.vector, "s": g.scalar, "t": g.tensor, "g": g, "y": g.sync}
    known = {q: {} for q in Q}
    count = {"cv": 0, "cs": 0, "ct": 0, "cg": 0}
    log = {}
    totals = {}
    nd = [0]

    def V(name, lo=0, hi=None, step=1, p=None):
        t = T[name]
        hi = t.shape[1] if hi is None else hi
        ps = slice(None) if p is None else slice(*p)
        return (t[ps, lo:hi] if step == 1 else t[ps, lo:hi:step], [(name, lo, hi)])

    def D(name, lo=0, hi=N):
        return (T[name][lo] if hi == lo + 1 else T[name][lo:hi], [(name, lo, hi)])

    def X(ap):
        return (ap, [])

    def G(win, off):
        return (win[0].indirect(off[0]), win[1] + off[1])

    def need(q, tok):
        sem, val, clock = tok
        if known[q].get(sem, 0) >= val:
            return
        Q[q].wait_ge(T.sem[sem], val)
        for s, v in clock.items():
            if known[q].get(s, 0) < v:
                known[q][s] = v
        known[q][sem] = val

    def order(q, reads, writes):
        toks = []
        for regs, wr in ((reads, False), (writes, True)):
            for name, lo, hi in regs:
                ps = name.startswith("ps")
                for (l2, h2, w2, q2, tok) in log.get(name, []):
                    if (q2 != q) if ps else ((wr or w2) and lo < h2 and l2 < hi):
                        toks.append(tok)
        toks.sort(key=lambda t: -t[1])
        for tok in toks:
            need(q, tok)

    def note(q, reads, writes, tok):
        for regs, wr in ((reads, False), (writes, True)):
            for name, lo, hi in regs:
                old = log.get(name, [])
                if wr and q != "dma" and not name.startswith("ps"):
                    old = [e for e in old if not (lo <= e[0] and e[1] <= hi)]
                old.append((lo, hi, wr, q, tok))
                log[name] = old

    def ap(v):
        return v[0] if isinstance(v, tuple) else v

    def run(q, out, ins, call):
        rd = [r for v in ins if isinstance(v, tuple) for r in v[1]]
        order(q, rd, out[1])
        sem = "c" + q
        call().then_inc(T.sem[sem], 1)
        count[sem] += 1
        note(q, rd, out[1], (sem, count[sem], dict(known[q])))

    def ts(out, x, s1, op0, s2=None, op1=None):
        if op1 is None:
            run("v", out, [x, s1], lambda: g.vector.tensor_scalar(out[0], x[0], ap(s1), None, op0))
        else:
            run("v", out, [x, s1, s2], lambda: g.vector.tensor_scalar(out[0], x[0], ap(s1), ap(s2), op0, op1))

    def tt(out, x, y, op):
        run("v", out, [x, y], lambda: g.vector.tensor_tensor(out[0], x[0], y[0], op))

    def cp(out, x):
        run("v", out, [x], lambda: g.vector.tensor_copy(out[0], x[0]))

    def ms(out, c):
        run("v", out, [], lambda: g.vector.memset(out[0], c))

    def act(out, x, scale=1.0, bias=0.0, func=AF.Identity):
        run("s", out, [x, scale, bias], lambda: g.scalar.activation(out[0], x[0], func, bias=ap(bias), scale=ap(scale)))

    def sel(out, x, pattern, op, fill_, base, ch):
        run("g", out, [x], lambda: g.affine_select(out[0], x[0], pattern, op, fill_, base, ch))

    def iota(out, pattern, base=0, ch=0):
        run("g", out, [], lambda: g.iota(out[0], pattern, base, ch, allow_small_or_imprecise_dtypes=True))

    def mm(items):
        rd = sorted(set(r for it in items for r in it[1][1] + it[2][1]))
        wr = sorted(set(r for it in items for r in it[0][1]))
        order("t", rd, wr)
        last = None
        for o, l, r, a, b in items:
            last = g.tensor.matmul(o[0], l[0], r[0], a, b)
        last.then_inc(T.sem["ct"], 1)
        count["ct"] += 1
        note("t", rd, wr, ("ct", count["ct"], dict(known["t"])))

    def dma(items):
        if not items:
            return
        sem = "d%d" % nd[0]
        nd[0] += 1
        clock = {}
        for q, o, i in items:
            order(q, i[1], o[1])
            Q[q].dma_start(o[0], i[0]).then_inc(T.sem[sem], 16)
            for s, v in known[q].items():
                clock[s] = max(v, clock.get(s, 0))
        totals[sem] = 16 * len(items)
        for q, o, i in items:
            note("dma", i[1], o[1], (sem, totals[sem], clock))

    masks = first_masks(core, T, topo, way)
    own = (16 * rank, 16 * rank + 16)

    def send(k):
        order("g", [("s_" + k, 0, N)], [])
        trs = []
        for j, b in enumerate(T.cores):
            if b == core:
                continue
            hop = way[core, b] if way[core, b] is not None else b
            rid, pid = topo.addr(hop, core)
            trs.append(RemoteDMATransfer(dst_ids=[DstId(rid=rid, pnc=pid)], dma_engine_mask=bits(masks[b]),
                                         remote_sem=T.sem["arr_" + k], src=T["s_" + k][j], dst=T["l_" + k][rank]))
        g.remote_dma_fused(trs, local_sem=T.sem["out_" + k])
        totals["out_" + k] = sum(len(m) for m in masks.values())

    def W(name):
        return (T[name], [(name, 0, T[name].shape[1])])

    def staged(k, t):
        dma([("y", D("s_" + k), (t[0][:], t[1]))])
        dma([("y", D("l_" + k, rank, rank + 1), (t[0][own[0]:own[1], :], t[1]))])

    def hand(k, src):
        hub = fan(core, T, topo, way)[0]
        es = topo.engines(core, hub)
        rid, pid = topo.addr(hub, core)
        order("g", src[1], [])
        g.remote_dma(T["l_" + k][rank], src[0], T.sem["arr_" + k], T.sem["out_" + k], pid, rid, bits(es))
        totals["out_" + k] = len(es)
        note("dma", src[1], [], ("out_" + k, len(es), dict(known["g"])))

    def rows_of(k):
        return (T["l_" + k][:, own[0]:own[1], :], [("l_" + k, 0, N)])

    near = [a for a in range(N) if way[T.cores[a], core] is None]
    late = [a for a in range(N) if a not in near]
    n_near = sum(len(first_masks(T.cores[a], T, topo, way)[core]) for a in near if a != rank)
    totals["far_b"] = sum(len(relay_engines(way[T.cores[a], core], core, topo)) for a in late)
    for k in MSG:
        totals["arr_" + k] = N if k in WHOLE else n_near if k == "b" else n_near + totals["far_b"]
        for a in range(N):
            if a != rank or k in WHOLE:
                sem = "far_b" if k == "b" and a in late else "arr_" + k
                note("far", [], [("l_" + k, a, a + 1)], (sem, totals[sem], {}))

    dma([("s", V("hx"), X(T.x0[:]))])
    dma([("y", V("hr"), X(T.rtab[:])), ("s", V("hn"), X(T.rn0[:]))])
    dma([("y", D("s_b"), X(T.btab[:]))])
    dma([("y", V("hi"), X(T.itab[:]))])
    dma([("y", V("hb"), X(T.btab[:]))])
    dma([("y", D("l_b", rank, rank + 1), X(T.btab[own[0]:own[1], :]))])

    run("g", V("pi", 0, 1), [], lambda: g.iota(T.pi[:, 0:1], [[0, 1]], 0, 1))
    iota(V("jj"), [[1, TW]])
    C_ = lambda i, p=None: V("col", i, i + 1, p=p)
    P_, R_, G16, ZC, WT, WT3, Z8C, GA, R64 = range(9)
    ms(V("rst"), 1.0)
    ms(V("lo"), -1.0)
    ms(V("ft", 0, Z0), 0.0)
    diag, grp = [[-1, 128]], [[16, 8], [0, 16]]
    ID = V("id1")
    sel(ID, V("rst", 0, 128), diag, A.is_equal, 0.0, 0, 1)
    sel(V("bo"), V("rst", 0, 128), [[-16, 8], [0, 16]], A.is_ge, 0.0, 0, 1)
    sel(V("bo"), V("bo"), grp, A.is_ge, 0.0, 15, -1)
    send("b")
    sel(V("lo"), V("lo"), grp, A.is_ge, 0.0, 15, -1)
    sel(V("lo"), V("lo"), diag, A.is_gt, 0.0, 0, 1)
    sel(V("lo"), V("lo"), diag, A.not_equal, -1024.0, 0, 1)
    ts(V("pi", 1, 2), V("pi", 0, 1), 15, A.bitwise_and)
    cp(C_(P_), V("pi", 0, 1))
    cp(C_(R_), V("pi", 1, 2))
    ts(C_(Z8C), C_(P_), 16.0, A.mult, 15.0, A.add)
    ts(V("mc"), V("jj", 0, 16), C_(R_), A.is_equal)
    ts(V("z8"), V("jj", 0, 144, p=(0, 8)), C_(Z8C, (0, 8)), A.is_equal, 1024.0, A.mult)
    ts(V("bc"), V("mc"), LOW, A.mult, -LOW, A.add)
    ts(V("et"), V("mc"), LOW, A.mult)
    tt(C_(G16), C_(P_), C_(R_), A.subtract)
    ts(C_(WT), C_(R_), 2048.0, A.mult, 1024.0, A.add)
    ts(C_(ZC), C_(G16), 15.0, A.add)
    ts(V("zs"), V("jj", 0, 144), C_(ZC), A.is_equal)
    ts(V("zw"), V("jj", 0, 144), C_(ZC), A.is_equal, C_(WT), A.mult)
    ts(V("fl"), V("jj", 0, 64), 16.0, A.mult, C_(R_), A.add)
    ts(V("fah"), V("fl"), float(N - rank), A.add, 1024.0, A.mult)

    def DG(c):
        i = DIAG.index(float(c))
        return V("dg", 128 * i, 128 * i + 128)

    def tblock(d):
        if d < 12:
            act(V("tm", d * TW, (d + 1) * TW), V("jj"), scale=V("mc", d, d + 1), bias=V("bc", d, d + 1))
        else:
            ts(V("tm", d * TW, (d + 1) * TW), V("jb"), V("mc", d, d + 1), A.mult, V("bc", d, d + 1), A.add)

    def lists(out, z, src, start=True, stop=True, h=None, at=None):
        lo, w = (0, 64) if h is None else (32 * h, 32)
        at = lo if at is None else at
        return [(V(out, at, at + w), V(z, 15 - r, 143 - r), V(src, 16 * lo + r, 16 * (lo + w), 16), start and r == 0, stop and r == 15)
                for r in range(16)]

    def rows(out, z, src):
        return [(V(out, 0, 64), V(z, 15 - r, 143 - r), V(src, 64 * r, 64 * r + 64), r == 0, r == 15) for r in range(16)]

    def part(name, i, n):
        w = F // n
        return V(name, w * i, w * i + w)

    def half(name, h):
        return part(name, h, 2)

    def quad(name, h):
        return V(name, 256 * h, 256 * h + 256)

    def offs(name, base, i, n):
        w = 64 // n
        return V(name, base + w * i, base + w * i + w)

    def key_lists():
        for i in range(2):
            ts(V("kb", 64 * i, 64 * i + 64), V("wki"), 2 + 4 * i, A.logical_shift_right, 15 * TW, A.bitwise_and)
        tt(V("kf"), V("kb"), V("fm"), A.add)
        cp(V("ko"), V("kf"))

    todo = []
    side = []

    def fill(n):
        while todo and (n > 0 or todo[0][2] == 0):
            job, lo, hi, uncut = todo[0]
            w = hi - lo if uncut else min(n, hi - lo)
            job(lo, lo + w)
            n -= w
            if lo + w == hi:
                todo.pop(0)
            else:
                todo[0] = (job, lo + w, hi, uncut)

    def later(job, w):
        todo.append((lambda lo, hi: job(), 0, w, True))

    def aside(n=1):
        for _ in range(n):
            if side:
                side.pop(0)()

    def far_lists(t, fa, out):
        C = B0 + t * F
        P = 1 << (C - 1).bit_length()
        H, S = V("psL0", 0, 64), V("psL1", 0, 64)
        tt(V("hv", 0, 64), H, V(fa), A.add)
        ts(V("hv", 64, 128), V("hv", 0, 64), 10, A.logical_shift_right, 7, A.bitwise_and)
        act(V("hf"), H, scale=1.0 / 1024.0)
        for i in range(2):
            act(V("hq", 64 * i, 64 * i + 64), H, scale=1.0 / (1024.0 * P), bias=FB - 0.5 + 0.5 / P + i * (P - C) / P)
        aside()
        for q in range(N):
            ts(V("oh", 64 * q, 64 * q + 64), V("hv", 64, 128), float(q), A.is_equal)
        mm([(V("psX%d" % h, 0, 256), V("lo"), quad("oh", h), True, False) for h in range(2)])
        run("v", V("sc"), [V("rst"), V("oh")], lambda: g.vector.tensor_tensor_scan(T.sc[:], T.rst[:], T.oh[:], 0.0, A.mult, A.add))
        for h in range(2):
            mm([(V("psX%d" % h, 0, 256), V("bo"), quad("sc", h), False, True)])
        mm([(S, V("idf"), V("hf"), True, False), (S, DG(C - P), V("hq", 0, 64), False, False), (S, DG(-C), V("hq", 64, 128), False, False)])
        fill(GAP[2])
        ts(quad("cm", 0), V("psX0", 0, 256), float(CAP - 1023), A.is_lt, 0.5, A.add)
        act(quad("cm", 1), V("psX1", 0, 256), scale=-1.0, bias=CAP - 1023.5, func=AF.Sign)
        mm([(S, DG(SLOT[q]), V("cm", 64 * q, 64 * q + 64), False, q == N - 1) for q in range(N)])
        fill(GAP[3])
        ts(out, S, Z0 - OK + FB * P - sum(SLOT[:4]) / 2 + sum(SLOT[4:]), A.add)

    def nothing(h):
        pass

    def walk(pick1, pick2, pre, conv1, conv2, old_win, bo):
        for h in range(2):
            pre(h)
            pick1(h, 2)
            mm(lists("psL%d" % h, "zs", "mr", start=pre is nothing, h=h, at=0))
        conv1(0)
        pre(0)
        pick2(0, 2)
        mm(lists("psL0", "zs", "mk", start=pre is nothing, h=0, at=0))
        conv1(1)
        pre(1)
        pick2(2, 4)
        conv2(0)
        aside()
        act(half("old", 0), G(old_win, offs(bo[0], bo[1], 0, 2)))
        pick2(3, 4)
        mm(lists("psL1", "zs", "mk", start=pre is nothing, h=1, at=0))
        mm(lists("psL0", "zw", "old", h=0))
        fill(GAP[0])
        conv2(1)
        cp(quad("old", 2), G(old_win, offs(bo[0], bo[1], 2, 4)))
        act(quad("old", 3), G(old_win, offs(bo[0], bo[1], 3, 4)))
        aside()
        mm(lists("psL0", "zw", "old", h=1))
        aside()
        fill(GAP[1])

    def fill_b(ranks, ks):
        items = []
        for k in ks:
            for a in ranks:
                if a - 1 in ranks and a != k:
                    continue
                n = 1
                while a + n in ranks and a + n != k:
                    n += 1
                p0 = 16 * ((a - k) % N)
                dst = V("ft", Z0 + k * CM, Z0 + k * CM + B0, p=(p0, p0 + 16 * n))[0]
                items.append(("y", (dst, [("ft", Z0 + k * CM + a, Z0 + k * CM + a + n)]), D("l_b", a, a + n)))
        dma(items)

    def fill_new(lo, w, ks):
        items = []
        for k in ks:
            c0 = Z0 + k * CM + lo
            items.append(("y", V("ft", c0, c0 + w, p=(0, 128 - 16 * k)), V("ft", Z0 + lo, Z0 + lo + w, p=(16 * k, 128))))
            items.append(("y", V("ft", c0, c0 + w, p=(128 - 16 * k, 128)), V("ft", Z0 + lo, Z0 + lo + w, p=(0, 16 * k))))
        dma(items)

    cp(half("hxb", 0), half("hx", 0))
    cp(V("e1", RN, RN + 64), V("hn"))
    cp(half("hxb", 1), half("hx", 1))
    mm(lists("psK", "z8", "hxb"))
    cp(V("e1", 0, R0), V("hr"))
    for d in range(0, 4):
        tblock(d)
    for h in range(2):
        act(half("p1", h), G(V("hr"), offs("e1", RN, h, 2)))
    cp(V("wki"), V("psK", 0, 64))
    ts(V("sb", 0, 64), V("wki"), 10, A.logical_shift_right, 15, A.bitwise_and)
    ts(V("sb", 64, 128), V("wki"), 14, A.logical_shift_right, 15, A.bitwise_and)
    cp(V("kd"), V("sb"))
    ts(V("e1", KY, KY + 64), V("psK", 0, 64), 1.0 / 1024.0, A.mult)
    staged("e", W("e1"))
    send("e")
    staged("t", X(T.itab))
    send("t")
    iota(V("fm"), [[0, 8], [16, 16]])
    for h in range(3):
        iota(V("cq", 64 * h, 64 * h + 64), [[-15 * TW * 2 ** h, 4], [0, 16]])
    for h in range(2):
        act(half("p2", h), G(V("et"), offs("kd", 64, h, 2)))
    for d in range(4, 8):
        tblock(d)
    later(lambda: [ts(DG(c), ID, float(c), A.mult) for c in [-512, -1536] + SLOT[:4]], GAP[0])
    later(lambda: [cp(V("idf"), ID)] + [ts(DG(c), ID, float(c), A.mult) for c in SLOT[4:]], GAP[1])
    walk(lambda i, n: tt(part("mr", i, n), G(V("et"), offs("kd", 0, i, n)), part("p1", i, n), A.min),
         lambda i, n: tt(part("mk", i, n), G(V("hi"), offs("j1", IO, i, n)), part("p2", i, n), A.min),
         nothing,
         lambda h: cp(offs("j1", IO, h, 2), V("psL%d" % h, 0, 32)),
         lambda h: cp(offs("j1", BO, h, 2), V("psL%d" % h, 0, 32)),
         V("hb"), ("j1", BO))
    hand("j", V("j1"))
    fill_b(near, range(EARLY[0]))
    ms(V("rst", 0, 512, 64), 0.0)
    far_lists(0, "fah", V("k1"))
    hand("k", V("k1"))
    cp(V("jb"), V("jj"))
    for d in range(8, 16):
        tblock(d)

    dma([("y", V("e2"), D("l_e"))])
    fill_b(late, [0])
    fill_b(near, range(EARLY[0], EARLY[1]))
    dma([("y", V("oi"), D("l_t"))])
    need("y", ("out_k", totals["out_k"], {}))
    dma([("y", V("j2"), rows_of("j"))])
    fill_b(late, range(1, EARLY[1]))
    fill_b(range(N), range(EARLY[1], N))
    dma([("y", V("k2"), rows_of("k"))])
    ts(V("fm"), V("fm"), C_(R_), A.add)
    ts(V("wki"), V("e2", KY, KY + 64), 1024.0, A.mult)
    key_lists()
    ts(C_(WT3), C_(R_), 6144.0, A.mult, 3072.0, A.add)
    ts(C_(GA), C_(G16), -64.0, A.mult, 8192.0, A.add)
    ts(C_(R64), C_(R_), 64.0, A.mult)
    ts(V("zw3"), V("jj", 0, 144), C_(ZC), A.is_equal, C_(WT3), A.mult)
    for c in (3, -2560, -3584, -4608):
        ts(DG(c), ID, float(c), A.mult)
    cp(V("idp"), ID)
    ts(V("idn"), ID, -1.0, A.mult)
    ts(V("fao"), V("fl"), 1024.0, A.mult, C_(GA), A.add)
    ts(V("fn"), V("jj", 0, 64), C_(R64), A.add)

    SCALE = (1.0, 1.0, 2.0, 4.0)
    BIAS = (0.0, 1024.0, 2048.0, 4096.0)
    RC = ("rt", "rca", "rcb", "rca")

    def mask_q(name, t, i):
        base = 0 if name == "p1" else 64
        act(quad(name, i), G(V("tm"), offs("ko", base, i, 4)), scale=SCALE[t], bias=BIAS[t] + SCALE[t] * TW * i)

    def it_window(t):
        return V("it", 0, I0 + 4096 if t == 3 else I0 + t * F)

    def root_append(t, off, base, n=8):
        todo.append((lambda a, b: tt(V(RC[t + 1], 128 * a, 128 * b), G(V(RC[t]), V(off, base + 8 * a, base + 8 * b)),
                                     V("p1", 128 * a, 128 * b), A.max), 0, n, False))

    def inner_append(t, off, base, n=8):
        def job(a, b):
            if t < 2:
                o = V("it", I0 + t * F + 128 * a, I0 + t * F + 128 * b)
            elif t == 2:
                o = V("it", I0 + 2048 + 256 * a, I0 + 2048 + 256 * b, 2)
            else:
                o = V("yu", 128 * a, 128 * b)
            tt(o, G(it_window(t), V(off, base + 8 * a, base + 8 * b)), V("p2", 128 * a, 128 * b), A.max)
        todo.append((job, 0, n, False))

    def side_append(win, off, p, m, out, a):
        lo = 128 * a
        ps = V("psQ", 0, F - lo)
        return [lambda: mm([(ps, V("idn"), V(m, lo), True, False), (ps, V("idp"), V(p, lo), False, False)]),
                lambda: act(V("gs", lo), G(win, V(off, 8 * a))),
                lambda: mm([(ps, V("idp"), V("gs", lo), False, True)]),
                lambda: act(V(out, lo), ps)]

    def finish(t, off):
        last = t == RO - 1
        C = B0 + t * F
        base = lambda b, h: (V("ps%s%d" % (b, h)), ID, half("old", h), True, False)
        far3 = lambda b, h, stop: (V("ps%s%d" % (b, h)), DG(3), half("far", h), False, stop)
        carry = lambda h: (V("psX%d" % h), ID, half("qn", h), False, True)
        mm([base("A", h) for h in range(2)])
        cp(half("far", 0), G(V("ft"), offs(off, 0, 0, 2)))
        act(half("far", 1), G(V("ft"), offs(off, 0, 1, 2)))
        mm([base("X", h) for h in range(2)] if last else lists("psK", "zw", "old", stop=False))
        for h in range(2):
            mm([far3("A", h, True)])
        mm([far3("X", h, False) for h in range(2)] if last else lists("psK", "zw3", "far", start=False))
        fill(GAP[4])
        qb = -(QB - 127.5 + t)
        ts(half("qn", 0), V("psA0"), -1.0, A.mult, qb, A.add)
        act(half("qn", 1), V("psA1"), scale=-1.0, bias=qb)
        if last:
            for h in range(2):
                mm([carry(h)])
            ts(half("yb_", 0), V("psX0"), QB + t, A.add)
            act(half("yb_", 1), V("psX1"), bias=QB + t)
            staged("y", W("yb_"))
            mm(rows("psQ", "zw", "yb_"))
            cp(V("wj"), V("psQ", 0, 64))
        else:
            mm(lists("psQ", "zw", "qn"))
            for h in range(2):
                mm([base("X", h), far3("X", h, False), carry(h)])
            fill(GAP[5])
            cp(V("wki"), V("psK", 0, 64))
            act(V("wkf"), V("psK", 0, 64), bias=1024.0 * 256.0 * (QB + t))
            key_lists()
            tt(V("wj"), V("psQ", 0, 64), V("wkf"), A.add)
        ts(V("sb", 0, 64), V("wj"), 13, A.logical_shift_right, F - 1, A.bitwise_and)
        ts(V("sb", 64, 128), V("wj"), 7 * 1024, A.bitwise_and)
        tt(V("sa", 0, 64), V("sb", 0, 64), V("sb", 64, 128), A.subtract)
        tt(V("sa", 64, 128), V("sb", 64, 128), V("fn" if last else "fl"), A.min)
        tt(V("sa", 128, 192), V("sa", 0, 64), V("sa", 64, 128), A.max)
        if last:
            ts(V("yn_"), V("sa", 128, 192), float(R0 + t * F), A.add)
            hand("n", V("yn_"))
            send("y")
            return
        fill(16)
        cp(V("so"), V("sa", 128, 192))
        for who, i in BETWEEN.split():
            i = int(i)
            if who in "12":
                mask_q("p" + who, t + 1, i)
                continue
            c0 = C + 512 * i
            if who == "n":
                act(V("ft", Z0 + c0, Z0 + c0 + 512), V("psX%d" % i), bias=QB + t)
            else:
                ts(V("ft", Z0 + c0, Z0 + c0 + 512), V("psX%d" % i), QB + t, A.add)
            if i:
                fill_new(C, F, [k for k in range(1, N) if k not in HALVES])
            fill_new(c0, 512, HALVES)

    for name in ("p1", "p2"):
        for i in range(4):
            mask_q(name, 0, i)
    ts(V("rt"), V("e2", 0, R0), float(-I0), A.add)
    root_append(0, "e2", RN)
    fill(4)
    fill(4)
    ts(V("it", 0, I0), V("oi"), float(-B0), A.add)
    for h in range(2):
        act(half("old", h), G(V("ft", Z0, Z0 + B0), offs("j2", BO, h, 2)))
    inner_append(0, "j2", IO)
    fill(4)
    fill(4)
    finish(0, "k2")

    for t in range(1, RO):
        low = 15.0 * (LOW * SCALE[t] - BIAS[t])
        last = t == RO - 1
        s0 = 64 * (t - 1)

        def pre(h):
            mm([(V("psL%d" % h, 0, 32), ID, V("cq", s0 + 32 * h, s0 + 32 * h + 32), True, False)])

        def conv2(h):
            L = V("psL%d" % h, 0, 32)
            if not last:
                ts(offs("bo_", 0, h, 2), L, low + B0, A.add)
            else:
                ts(V("sa", 0, 32), L, low + B0, A.add)
                ts(V("sa", 64, 96), L, low + 5120.0, A.add, 0.5, A.mult)
                tt(V("sa", 128, 160), V("sa", 0, 32), V("sa", 64, 96), A.min)
                cp(offs("bo_", 0, h, 2), V("sa", 128, 160))

        if not last:
            root_append(t, "so", 0, NV_ROOT)
            inner_append(t, "io_", 0)
            side.extend(side_append(V(RC[t]), "so", "p1", "mr", RC[t + 1], NV_ROOT))
        else:
            inner_append(t, "io_", 0, NV_LAST)
            later(lambda: (staged("i", W("yu")), send("i")), 0)
            st = side_append(it_window(t), "io_", "p2", "mk", "yu", NV_LAST)
            side.extend([lambda: None, lambda: (st[0](), st[1]()), lambda: (st[2](), st[3]())])
        walk(lambda i, n: tt(part("mr", i, n), G(V(RC[t]), offs("so", 0, i, n)), part("p1", i, n), A.min),
             lambda i, n: tt(part("mk", i, n), G(it_window(t), offs("io_", 0, i, n)), part("p2", i, n), A.min),
             pre,
             lambda h: ts(offs("io_", 0, h, 2), V("psL%d" % h, 0, 32), low + I0, A.add),
             conv2, V("ft", Z0, Z0 + B0 + t * F), ("bo_", 0))
        far_lists(t, "fao", V("fo"))
        finish(t, "fo")

    dma([("y", V("yu"), D("l_i"))])
    dma([("y", X(T.yn[:]), rows_of("n"))])
    dma([("y", X(T.yb[:]), D("l_y"))])
    for i, bank in enumerate(("psA0", "psX0", "psA1", "psX1")):
        ps = V(bank, 0, 256)
        ts(quad("p1", i), quad("yu", i), 0.5, A.mult, 1024.0, A.max)
        ts(quad("p2", i), quad("yu", i), 0.25, A.mult, 1024.0, A.max)
        mm([(ps, V("idp"), quad("yu", i), True, False), (ps, V("idn"), quad("p1", i), False, False), (ps, V("idn"), quad("p2", i), False, True)])
        act(quad("rca", i), ps, bias=B0 + 2048.0)
        if i % 2:
            dma([("s", X(T.yi[:, 256 * i - 256:256 * i + 256]), half("rca", i // 2))])
    totals.update(count)
    for sem, val in totals.items():
        need("g", (sem, val, {}))
